import numpy as np
import ml_dtypes


def mxq(x, axis, fmt="e4m3"):
    dtype, down = {"e4m3": (ml_dtypes.float8_e4m3fn, 7), "e5m2": (ml_dtypes.float8_e5m2, 14)}[fmt]
    v = np.moveaxis(np.asarray(x, np.float32).astype(ml_dtypes.bfloat16).astype(np.float64), axis, -1)
    blocks = v.reshape(v.shape[:-1] + (-1, 32))
    amax = np.abs(blocks).max(-1, keepdims=True)
    byte = np.maximum(np.where(amax > 0, np.frexp(amax)[1] - 1 + 127, 0) - down, 1)
    scale = np.exp2(byte - 127.0)
    codes = (blocks / scale).astype(np.float32).astype(dtype).astype(np.float64)
    return np.moveaxis((codes * scale).reshape(v.shape), -1, axis)


WIDE = False


def mx_kscale(k):
    if not WIDE:
        return np.ones(k)
    levels = np.array([10, -10, 5, -5, 0])
    if k % 512:
        return np.exp2(np.random.permutation(np.resize(levels, k // 32))).repeat(32)
    a = np.empty((k // 512, 16))
    for p in range(k // 512):
        a[p, :8] = np.random.permutation(np.resize(levels, 8))
        for g in range(8):
            far = levels[np.abs(levels - a[p, g]) >= 10]
            a[p, g + 8] = far[np.random.randint(len(far))]
    return np.exp2(a.ravel()).repeat(32)


def f64(x):
    return np.asarray(x).astype(np.float64)


def striped(idx):
    return np.tile(idx.reshape(-1, 16).T, (8, 1)).astype(np.uint16)


def unstriped(offs):
    return offs[:16].T.reshape(-1).astype(np.int64)


def pack_weight(w):
    k, n = w.shape
    w = f64(np.asarray(w, np.float32).astype(ml_dtypes.bfloat16)).reshape(k // 32, 32, n)
    amax = np.abs(w).max(1)
    byte = np.clip(np.where(amax > 0, np.frexp(amax)[1] - 1 + 127 - 7, 1), 1, 254)
    scaled = (w * np.exp2(127.0 - byte)[:, None, :]).reshape(k, n).astype(np.float32)
    words = np.ascontiguousarray(scaled.reshape(k // 512, 128, 4, n).transpose(0, 1, 3, 2)).astype(ml_dtypes.float8_e4m3fn).view(np.uint8)
    return words, np.ascontiguousarray(byte.astype(np.uint8).reshape(k // 512, 16, n))


def unpack_weight(words, scales):
    g, p, n, _ = words.shape
    vals = np.ascontiguousarray(words).view(ml_dtypes.float8_e4m3fn).astype(np.float64) * np.repeat(np.exp2(scales.astype(np.float64) - 127.0), 8, axis=1)[..., None]
    return vals.transpose(0, 1, 3, 2).reshape(g * 512, n)


def relu(v):
    return np.maximum(v, 0.0)


K, T, S, N = 512, 2048, 1024, 256


def setup_inputs():
    n = np.random.standard_normal
    s = mx_kscale(K)[:, None]
    packed_w1 = pack_weight(n((K, N)) / np.sqrt(3 * K) / s)
    packed_w2 = pack_weight(n((K, N)) / np.sqrt(3 * K) / s)
    packed_w3 = pack_weight(n((K, N)) / np.sqrt(3 * K) / s)
    return {
        "xT": (n((K, T)) * s).astype(np.float32),
        "w1_words": packed_w1[0],
        "w1_scales": packed_w1[1],
        "w2_words": packed_w2[0],
        "w2_scales": packed_w2[1],
        "w3_words": packed_w3[0],
        "w3_scales": packed_w3[1],
        "offs": striped(np.random.permutation(T)[:S]),
    }


def reference(xT, w1_words, w1_scales, w2_words, w2_scales, w3_words, w3_scales, offs):
    xq = mxq(f64(xT)[:, unstriped(offs)], 0, "e4m3")
    y0 = unpack_weight(w1_words, w1_scales).T @ xq
    y1 = unpack_weight(w2_words, w2_scales).T @ xq
    y2 = unpack_weight(w3_words, w3_scales).T @ xq
    return relu(y0 + np.pad(y1, ((0, 0), (1, 0)))[:, :S] + np.pad(y2, ((0, 0), (2, 0)))[:, :S])

@@ -1,0 +1,214 @@
+from contextlib import ExitStack
+
+import concourse.mybir as mybir
+
+K, T, S, N = 512, 2048, 1024, 256
+TAPS = 3
+FLOPS = 2 * TAPS * K * N * S
+
+F32 = mybir.dt.float32
+BF16 = mybir.dt.bfloat16
+I32 = mybir.dt.int32
+U32 = mybir.dt.uint32
+U16 = mybir.dt.uint16
+U8 = mybir.dt.uint8
+FP8X4 = mybir.dt.float8_e4m3fn_x4
+COPY = mybir.ActivationFunctionType.Copy
+RELU = mybir.ActivationFunctionType.Relu
+
+P = 128
+SLICE = 256
+SLICES = S // SLICE
+HALF = SLICE // 2
+WORD_PAD = 16
+BYTE_PAD = 64
+WARM = 6
+
+LOADS = (((0, 1024), (1024, 1536), (1536, 2048)),
+         ((0, 512), (512, 1024), (1024, 1536), (1536, 1792), (1792, 2048)))
+SCALAR_COLS = ((384, 128, 128), (512, 512, 0, 64, 96))
+VECTOR_WEAVES = (0,)
+
+
+def tile_picked_listconv_relu_e_kernel(
+    tc, xT, w1_words, w1_scales, w2_words, w2_scales, w3_words, w3_scales, offs, out
+):
+    nc = tc.nc
+    words_in = (w1_words, w2_words, w3_words)
+    scales_in = (w1_scales, w2_scales, w3_scales)
+    x_rows = xT.rearrange("(p j) t -> p j t", j=4)
+    out_rows = out.rearrange("(m p) s -> p m s", p=P)
+
+    with ExitStack() as ctx:
+        keep = ctx.enter_context(tc.tile_pool(name="keep", bufs=1))
+        psum = ctx.enter_context(tc.psum_pool(name="psum", bufs=1))
+
+        offsets = keep.tile([P, S // 16], U16, name="offsets")
+        w_codes = [keep.tile([P, N], U32, name="w_codes%d" % d, align_bytes=64) for d in range(TAPS)]
+        w_scales = keep.tile([P, TAPS * N], U8, name="w_scales", align_bytes=64)
+        raw = [[keep.tile([P, 2, c1 - c0], F32, name="raw%d_%d" % (u, c0)) for c0, c1 in LOADS[u]] for u in range(2)]
+        pairs = [keep.tile([P, 2 * T], BF16, name="pairs%d" % u) for u in range(2)]
+        codes = keep.tile([P, 2, WORD_PAD + S // 2], U32, name="codes", align_bytes=64)
+        scales = keep.tile([P, 2, BYTE_PAD + S // 2], U8, name="scales", align_bytes=64)
+
+        nc.gpsimd.memset(w_scales[:].bitcast(I32), 0)
+        nc.gpsimd.memset(scales[:].rearrange("p r c -> p (r c)").bitcast(I32), 0)
+        nc.gpsimd.memset(codes[:, :, 0:WORD_PAD].bitcast(I32), 0)
+
+        def load_x(u, i):
+            c0, c1 = LOADS[u][i]
+            nc.sync.dma_start(out=raw[u][i][:], in_=x_rows[:, 2 * u : 2 * u + 2, c0:c1])
+
+        def load_scale(n):
+            d, q = divmod(n, 4)
+            nc.sync.dma_start(
+                out=w_scales[32 * q : 32 * q + 4, d * N : (d + 1) * N].bitcast(I32),
+                in_=scales_in[d][0, 4 * q : 4 * q + 4, :].bitcast(I32),
+            )
+
+        def load_w(d):
+            nc.sync.dma_start(
+                out=w_codes[d][:].bitcast(I32),
+                in_=words_in[d][0].rearrange("p n t -> p (n t)").bitcast(I32),
+            )
+
+        load_x(0, 0)
+        nc.sync.dma_start(offsets[:], offs)
+        for n in range(0, 4):
+            load_scale(n)
+        load_x(0, 1)
+        load_x(0, 2)
+        load_x(1, 0)
+        for n in range(4, 9):
+            load_scale(n)
+        load_x(1, 1)
+        load_x(1, 2)
+        load_x(1, 3)
+        for n in range(9, 12):
+            load_scale(n)
+        load_x(1, 4)
+        for d in range(TAPS):
+            load_w(d)
+
+        def round_pairs(u, i):
+            c0, c1 = LOADS[u][i]
+            cut = SCALAR_COLS[u][i]
+            for a, b, on_scalar in ((0, cut, True), (cut, c1 - c0, False)):
+                if a == b:
+                    continue
+                dst = pairs[u][:, 2 * (c0 + a) : 2 * (c0 + b)].rearrange("p (c i t) -> p c t i", i=4, t=2)
+                src = raw[u][i][:, :, a:b].rearrange("p t (c i) -> p c t i", i=4)
+                if on_scalar:
+                    nc.scalar.activation(dst, src, COPY)
+                else:
+                    nc.vector.tensor_copy(dst, src)
+
+        grouped = [keep.tile([P, 4 * SLICE], BF16, name="grouped%d" % s, align_bytes=64) for s in range(SLICES)]
+        picked = {s: keep.tile([P, 2, SLICE], U32, name="picked%d" % s) for s in range(SLICES) if s not in VECTOR_WEAVES}
+
+        def gather(u, s):
+            window = pairs[u][:].bitcast(U32).indirect(offsets[:, 16 * s : 16 * (s + 1)])
+            if s in VECTOR_WEAVES:
+                dst = grouped[s][:].bitcast(U32).rearrange("p (r c u) -> p u c r", r=2, u=2)[:, u]
+            else:
+                dst = picked[s][:, u, :]
+            nc.vector.tensor_copy(dst, window)
+
+        def weave(s):
+            if s not in VECTOR_WEAVES:
+                nc.scalar.copy(
+                    grouped[s][:].bitcast(U32).rearrange("p (r c u) -> p r c u", r=2, u=2),
+                    picked[s][:].rearrange("p u (c r) -> p r c u", r=2),
+                )
+
+        def quantise(s):
+            for r in (1, 0):
+                nc.vector.quantize_mx(
+                    out=codes[:, r, WORD_PAD + HALF * s : WORD_PAD + HALF * (s + 1)].bitcast(FP8X4),
+                    scales=scales[:, r, BYTE_PAD + HALF * s : BYTE_PAD + HALF * (s + 1)],
+                    in_=grouped[s][:, 4 * HALF * r : 4 * HALF * (r + 1)],
+                )
+
+        late_codes = [keep.tile([P, 2, HALF], U32, name="late_codes%d" % s, align_bytes=64) for s in range(SLICES)]
+        late_scales = [keep.tile([P, 2, HALF], U8, name="late_scales%d" % s, align_bytes=64) for s in range(SLICES)]
+
+        def shift(s):
+            w0 = WORD_PAD + HALF * s - 1
+            b0 = BYTE_PAD + HALF * s - 1
+            nc.vector.tensor_copy(late_codes[s][:], codes[:, :, w0 : w0 + HALF])
+            nc.vector.tensor_copy(late_scales[s][:], scales[:, :, b0 : b0 + HALF])
+
+        banks = [psum.tile([P, 512], F32, name="bank%d" % b) for b in range(8)]
+
+        def one_pass(s, m, r, d):
+            src_phase = (r - d) % 2
+            if r - d >= 0:
+                rhs = codes[:, src_phase, WORD_PAD + HALF * s : WORD_PAD + HALF * (s + 1)]
+                rhs_scale = scales[:, src_phase, BYTE_PAD + HALF * s : BYTE_PAD + HALF * (s + 1)]
+            else:
+                rhs = late_codes[s][:, src_phase, :]
+                rhs_scale = late_scales[s][:, src_phase, :]
+            nc.tensor.matmul_mx(
+                out=banks[2 * s + m][:, HALF * r : HALF * (r + 1)],
+                lhsT=w_codes[d][:, P * m : P * (m + 1)].bitcast(FP8X4),
+                lhsT_scale=w_scales[:, d * N + P * m : d * N + P * (m + 1)],
+                rhs=rhs.bitcast(FP8X4),
+                rhs_scale=rhs_scale,
+                start=(d == 0),
+                stop=(d == TAPS - 1),
+            )
+
+        def multiply(s):
+            for m in range(2):
+                for d in range(2):
+                    one_pass(s, m, 1, d)
+            for m in range(2):
+                one_pass(s, m, 1, 2)
+                for d in range(TAPS):
+                    one_pass(s, m, 0, d)
+
+        def finish(s):
+            for m in range(2):
+                result = keep.tile([P, SLICE], F32, name="result%d_%d" % (s, m))
+                src = banks[2 * s + m][:, 0:SLICE].rearrange("p (r c) -> p c r", r=2)
+                dst = result[:].rearrange("p (c r) -> p c r", r=2)
+                if s == SLICES - 1 and m == 0:
+                    nc.vector.tensor_scalar_max(dst, src, 0.0)
+                else:
+                    nc.scalar.activation(dst, src, RELU)
+                nc.sync.dma_start(out=out_rows[:, m, SLICE * s : SLICE * (s + 1)], in_=result[:])
+
+        for i in range(len(LOADS[0])):
+            round_pairs(0, i)
+        for s in range(SLICES):
+            gather(0, s)
+        for i in range(len(LOADS[1])):
+            round_pairs(1, i)
+
+        for i in range(WARM):
+            nc.tensor.matmul_mx(
+                out=banks[7][:, 256:512],
+                lhsT=w_codes[0][:, 0:P].bitcast(FP8X4),
+                lhsT_scale=w_scales[:, 0:P],
+                rhs=w_codes[0][:].bitcast(FP8X4),
+                rhs_scale=w_scales[:, 0:N],
+                start=True,
+                stop=True,
+            )
+
+        gather(1, 0)
+        gather(1, 1)
+        weave(1)
+        quantise(0)
+        gather(1, 2)
+        weave(2)
+        shift(0)
+        multiply(0)
+        gather(1, 3)
+        weave(3)
+        finish(0)
+        for s in range(1, SLICES):
+            quantise(s)
+            shift(s)
+            multiply(s)
+            finish(s)

@@ -19,15 +19,16 @@ RELU = mybir.ActivationFunctionType.Relu
 P = 128
 SLICE = 256
 SLICES = S // SLICE
-HALF = SLICE // 2
-WORD_PAD = 16
-BYTE_PAD = 64
-WARM = 6
+PHASES = 4
+COLS = SLICE // PHASES
+HALO = TAPS - 1
+ROWS = HALO + PHASES
 
-LOADS = (((0, 1024), (1024, 1536), (1536, 2048)),
-         ((0, 512), (512, 1024), (1024, 1536), (1536, 1792), (1792, 2048)))
-SCALAR_COLS = ((384, 128, 128), (512, 512, 0, 64, 96))
-VECTOR_WEAVES = (0,)
+LOADS = (((0, 1024), (1024, 2048)),
+         ((0, 1024), (1024, 1536), (1536, 1792), (1792, 2048)))
+SPLIT = (0, 3)
+WARM = 3
+SCALAR_COLS = ((384, 384), (512, 256, 96, 96))
 
 
 def tile_picked_listconv_relu_e_kernel(
@@ -44,58 +45,58 @@ def tile_picked_listconv_relu_e_kernel(
         psum = ctx.enter_context(tc.psum_pool(name="psum", bufs=1))
 
         offsets = keep.tile([P, S // 16], U16, name="offsets")
-        w_codes = [keep.tile([P, N], U32, name="w_codes%d" % d, align_bytes=64) for d in range(TAPS)]
+        w_codes = keep.tile([P, TAPS * N], U32, name="w_codes", align_bytes=64)
         w_scales = keep.tile([P, TAPS * N], U8, name="w_scales", align_bytes=64)
         raw = [[keep.tile([P, 2, c1 - c0], F32, name="raw%d_%d" % (u, c0)) for c0, c1 in LOADS[u]] for u in range(2)]
         pairs = [keep.tile([P, 2 * T], BF16, name="pairs%d" % u) for u in range(2)]
-        codes = keep.tile([P, 2, WORD_PAD + S // 2], U32, name="codes", align_bytes=64)
-        scales = keep.tile([P, 2, BYTE_PAD + S // 2], U8, name="scales", align_bytes=64)
+        picked = keep.tile([P, 7 * SLICE], U32, name="picked")
+        grouped = [keep.tile([P, 4 * SLICE], BF16, name="grouped%d" % s, align_bytes=64) for s in range(SLICES)]
+        codes = [keep.tile([P, ROWS * COLS], U32, name="codes%d" % s, align_bytes=64) for s in range(SLICES)]
+        scales = [keep.tile([P, ROWS * COLS], U8, name="scales%d" % s, align_bytes=64) for s in range(SLICES)]
+        results = [keep.tile([P, 2, SLICE], F32, name="result%d" % s) for s in range(SLICES)]
+        banks = [psum.tile([P, 512], F32, name="bank%d" % b) for b in range(2 * SLICES)]
 
-        nc.gpsimd.memset(w_scales[:].bitcast(I32), 0)
-        nc.gpsimd.memset(scales[:].rearrange("p r c -> p (r c)").bitcast(I32), 0)
-        nc.gpsimd.memset(codes[:, :, 0:WORD_PAD].bitcast(I32), 0)
+        nc.vector.memset(w_scales[:].bitcast(I32), 0)
+        for s in range(SLICES):
+            nc.vector.memset(scales[s][:].bitcast(I32), 0)
+        nc.vector.memset(codes[0][:].bitcast(I32).rearrange("p (r c) -> p r c", c=COLS)[:, 0:HALO, 0:1], 0)
 
         def load_x(u, i):
             c0, c1 = LOADS[u][i]
             nc.sync.dma_start(out=raw[u][i][:], in_=x_rows[:, 2 * u : 2 * u + 2, c0:c1])
 
-        def load_scale(n):
+        def load_scale(n, queue=nc.sync):
             d, q = divmod(n, 4)
-            nc.sync.dma_start(
+            queue.dma_start(
                 out=w_scales[32 * q : 32 * q + 4, d * N : (d + 1) * N].bitcast(I32),
                 in_=scales_in[d][0, 4 * q : 4 * q + 4, :].bitcast(I32),
             )
 
         def load_w(d):
             nc.sync.dma_start(
-                out=w_codes[d][:].bitcast(I32),
+                out=w_codes[:, d * N : (d + 1) * N].bitcast(I32),
                 in_=words_in[d][0].rearrange("p n t -> p (n t)").bitcast(I32),
             )
 
         load_x(0, 0)
         nc.sync.dma_start(offsets[:], offs)
-        for n in range(0, 4):
+        for n in range(4, 8):
+            load_scale(n, nc.gpsimd)
+        for n in range(8, 12):
             load_scale(n)
         load_x(0, 1)
-        load_x(0, 2)
-        load_x(1, 0)
-        for n in range(4, 9):
+        for i in range(4):
+            load_x(1, i)
+        load_w(1)
+        load_w(2)
+        for n in range(0, 4):
             load_scale(n)
-        load_x(1, 1)
-        load_x(1, 2)
-        load_x(1, 3)
-        for n in range(9, 12):
-            load_scale(n)
-        load_x(1, 4)
-        for d in range(TAPS):
-            load_w(d)
+        load_w(0)
 
         def round_pairs(u, i):
             c0, c1 = LOADS[u][i]
             cut = SCALAR_COLS[u][i]
             for a, b, on_scalar in ((0, cut, True), (cut, c1 - c0, False)):
-                if a == b:
-                    continue
                 dst = pairs[u][:, 2 * (c0 + a) : 2 * (c0 + b)].rearrange("p (c i t) -> p c t i", i=4, t=2)
                 src = raw[u][i][:, :, a:b].rearrange("p t (c i) -> p c t i", i=4)
                 if on_scalar:
@@ -103,112 +104,124 @@ def tile_picked_listconv_relu_e_kernel(
                 else:
                     nc.vector.tensor_copy(dst, src)
 
-        grouped = [keep.tile([P, 4 * SLICE], BF16, name="grouped%d" % s, align_bytes=64) for s in range(SLICES)]
-        picked = {s: keep.tile([P, 2, SLICE], U32, name="picked%d" % s) for s in range(SLICES) if s not in VECTOR_WEAVES}
+        picked_row = ((2, 3, 0, 1), (4, 5, 6, 3))
 
-        def gather(u, s):
-            window = pairs[u][:].bitcast(U32).indirect(offsets[:, 16 * s : 16 * (s + 1)])
-            if s in VECTOR_WEAVES:
-                dst = grouped[s][:].bitcast(U32).rearrange("p (r c u) -> p u c r", r=2, u=2)[:, u]
-            else:
-                dst = picked[s][:, u, :]
-            nc.vector.tensor_copy(dst, window)
+        def gather(u, s, count):
+            window = pairs[u][:].bitcast(U32).indirect(offsets[:, 16 * s : 16 * (s + count)])
+            a = picked_row[u][s] * SLICE
+            nc.vector.tensor_copy(picked[:, a : a + count * SLICE], window)
 
         def weave(s):
-            if s not in VECTOR_WEAVES:
-                nc.scalar.copy(
-                    grouped[s][:].bitcast(U32).rearrange("p (r c u) -> p r c u", r=2, u=2),
-                    picked[s][:].rearrange("p u (c r) -> p r c u", r=2),
-                )
+            r0, r1 = picked_row[0][s], picked_row[1][s]
+            both = picked[:].rearrange("p (k j) -> p k j", j=SLICE)[:, r0 : r1 + 1 : r1 - r0, :]
+            copy = nc.vector.tensor_copy if s == SLICES - 1 else nc.scalar.copy
+            copy(
+                grouped[s][:].bitcast(U32).rearrange("p (r c u) -> p c r u", r=PHASES, u=2),
+                both.rearrange("p u (c r) -> p c r u", r=PHASES),
+            )
 
         def quantise(s):
-            for r in (1, 0):
+            for r in (2, 0):
+                cols = slice((HALO + r) * COLS, (HALO + r + 2) * COLS)
                 nc.vector.quantize_mx(
-                    out=codes[:, r, WORD_PAD + HALF * s : WORD_PAD + HALF * (s + 1)].bitcast(FP8X4),
-                    scales=scales[:, r, BYTE_PAD + HALF * s : BYTE_PAD + HALF * (s + 1)],
-                    in_=grouped[s][:, 4 * HALF * r : 4 * HALF * (r + 1)],
+                    out=codes[s][:, cols].bitcast(FP8X4),
+                    scales=scales[s][:, cols],
+                    in_=grouped[s][:, 4 * COLS * r : 4 * COLS * (r + 2)],
                 )
 
-        late_codes = [keep.tile([P, 2, HALF], U32, name="late_codes%d" % s, align_bytes=64) for s in range(SLICES)]
-        late_scales = [keep.tile([P, 2, HALF], U8, name="late_scales%d" % s, align_bytes=64) for s in range(SLICES)]
+        def rows_of(tile):
+            return tile[:].rearrange("p (r c) -> p r c", c=COLS)
 
         def shift(s):
-            w0 = WORD_PAD + HALF * s - 1
-            b0 = BYTE_PAD + HALF * s - 1
-            nc.vector.tensor_copy(late_codes[s][:], codes[:, :, w0 : w0 + HALF])
-            nc.vector.tensor_copy(late_scales[s][:], scales[:, :, b0 : b0 + HALF])
+            for tiles in (codes, scales):
+                rows = rows_of(tiles[s])
+                nc.vector.tensor_copy(rows[:, 0:HALO, 1:COLS], rows[:, PHASES:ROWS, 0 : COLS - 1])
 
-        banks = [psum.tile([P, 512], F32, name="bank%d" % b) for b in range(8)]
+        def carry(s):
+            for tiles in (codes, scales):
+                nc.vector.tensor_copy(
+                    rows_of(tiles[s + 1])[:, 0:HALO, 0:1], rows_of(tiles[s])[:, PHASES:ROWS, COLS - 1 : COLS]
+                )
 
-        def one_pass(s, m, r, d):
-            src_phase = (r - d) % 2
-            if r - d >= 0:
-                rhs = codes[:, src_phase, WORD_PAD + HALF * s : WORD_PAD + HALF * (s + 1)]
-                rhs_scale = scales[:, src_phase, BYTE_PAD + HALF * s : BYTE_PAD + HALF * (s + 1)]
-            else:
-                rhs = late_codes[s][:, src_phase, :]
-                rhs_scale = late_scales[s][:, src_phase, :]
+        def one_pass(s, m, d, r, count, start, stop):
+            a = (HALO - d + r) * COLS
+            cols = slice(a, a + count * COLS)
+            w_cols = slice(d * N + P * m, d * N + P * (m + 1))
             nc.tensor.matmul_mx(
-                out=banks[2 * s + m][:, HALF * r : HALF * (r + 1)],
-                lhsT=w_codes[d][:, P * m : P * (m + 1)].bitcast(FP8X4),
-                lhsT_scale=w_scales[:, d * N + P * m : d * N + P * (m + 1)],
-                rhs=rhs.bitcast(FP8X4),
-                rhs_scale=rhs_scale,
-                start=(d == 0),
-                stop=(d == TAPS - 1),
+                out=banks[2 * s + m][:, r * COLS : (r + count) * COLS],
+                lhsT=w_codes[:, w_cols].bitcast(FP8X4),
+                lhsT_scale=w_scales[:, w_cols],
+                rhs=codes[s][:, cols].bitcast(FP8X4),
+                rhs_scale=scales[s][:, cols],
+                start=start,
+                stop=stop,
             )
 
         def multiply(s):
-            for m in range(2):
-                for d in range(2):
-                    one_pass(s, m, 1, d)
-            for m in range(2):
-                one_pass(s, m, 1, 2)
-                for d in range(TAPS):
-                    one_pass(s, m, 0, d)
+            if s in SPLIT:
+                for m in range(2):
+                    one_pass(s, m, 0, 0, PHASES, True, False)
+                    for d in range(1, TAPS):
+                        one_pass(s, m, d, 2, 2, False, False)
+                for m in range(2):
+                    for d in range(1, TAPS):
+                        one_pass(s, m, d, 0, 2, False, d == TAPS - 1)
+            else:
+                for m in range(2):
+                    one_pass(s, m, 0, 0, PHASES, True, False)
+                for m in range(2):
+                    for d in range(1, TAPS):
+                        one_pass(s, m, d, 0, PHASES, False, d == TAPS - 1)
+
+        def relu(s, m, on_vector):
+            src = banks[2 * s + m][:, 0:SLICE].rearrange("p (r c) -> p c r", r=PHASES)
+            dst = results[s][:, m, :].rearrange("p (c r) -> p c r", r=PHASES)
+            if on_vector:
+                nc.vector.tensor_scalar_max(dst, src, 0.0)
+            else:
+                nc.scalar.activation(dst, src, RELU)
 
         def finish(s):
-            for m in range(2):
-                result = keep.tile([P, SLICE], F32, name="result%d_%d" % (s, m))
-                src = banks[2 * s + m][:, 0:SLICE].rearrange("p (r c) -> p c r", r=2)
-                dst = result[:].rearrange("p (c r) -> p c r", r=2)
-                if s == SLICES - 1 and m == 0:
-                    nc.vector.tensor_scalar_max(dst, src, 0.0)
-                else:
-                    nc.scalar.activation(dst, src, RELU)
-                nc.sync.dma_start(out=out_rows[:, m, SLICE * s : SLICE * (s + 1)], in_=result[:])
+            cols = slice(SLICE * s, SLICE * (s + 1))
+            if s < SLICES - 1:
+                for m in range(2):
+                    relu(s, m, False)
+                nc.sync.dma_start(out=out_rows[:, :, cols], in_=results[s][:])
+            else:
+                relu(s, 0, False)
+                nc.scalar.dma_start(out=out_rows[:, 0, cols], in_=results[s][:, 0, :])
+                relu(s, 1, True)
+                nc.sync.dma_start(out=out_rows[:, 1, cols], in_=results[s][:, 1, :])
 
         for i in range(len(LOADS[0])):
             round_pairs(0, i)
-        for s in range(SLICES):
-            gather(0, s)
+        for s in range(0, SLICES, 2):
+            gather(0, s, 2)
         for i in range(len(LOADS[1])):
             round_pairs(1, i)
 
         for i in range(WARM):
             nc.tensor.matmul_mx(
-                out=banks[7][:, 256:512],
-                lhsT=w_codes[0][:, 0:P].bitcast(FP8X4),
-                lhsT_scale=w_scales[:, 0:P],
-                rhs=w_codes[0][:].bitcast(FP8X4),
-                rhs_scale=w_scales[:, 0:N],
+                out=banks[7][:],
+                lhsT=w_codes[:, N : N + P].bitcast(FP8X4),
+                lhsT_scale=w_scales[:, N : N + P],
+                rhs=w_codes[:, N : 3 * N].bitcast(FP8X4),
+                rhs_scale=w_scales[:, N : 3 * N],
                 start=True,
                 stop=True,
             )
 
-        gather(1, 0)
-        gather(1, 1)
-        weave(1)
-        quantise(0)
-        gather(1, 2)
-        weave(2)
-        shift(0)
-        multiply(0)
-        gather(1, 3)
-        weave(3)
-        finish(0)
-        for s in range(1, SLICES):
+        for s in range(3):
+            gather(1, s, 1)
+            weave(s)
+        for s in range(SLICES):
             quantise(s)
             shift(s)
             multiply(s)
+            if s + 1 < SLICES:
+                carry(s)
+            if s == 1:
+                gather(1, 3, 1)
+            if s == 2:
+                weave(3)
             finish(s)

@@ -24,11 +24,13 @@ COLS = SLICE // PHASES
 HALO = TAPS - 1
 ROWS = HALO + PHASES
 
-LOADS = (((0, 1024), (1024, 2048)),
-         ((0, 1024), (1024, 1536), (1536, 1792), (1792, 2048)))
+PAIR_LOADS = ((0, 1024), (1024, 1536), (1536, 2048))
+PAIR_SCALAR_COLS = (0, 0, 0)
+ROW2_SCALAR_COLS = 640
+ROW3_LOADS = ((0, 512), (512, 1024), (1024, 1536), (1536, 1792), (1792, 2048))
 SPLIT = (0, 3)
-WARM = 3
-SCALAR_COLS = ((384, 384), (512, 256, 96, 96))
+WARM = 2
+VECTOR_RELU = ((1, 1), (2, 1), (3, 1))
 
 
 def tile_picked_listconv_relu_e_kernel(
@@ -47,23 +49,29 @@ def tile_picked_listconv_relu_e_kernel(
         offsets = keep.tile([P, S // 16], U16, name="offsets")
         w_codes = keep.tile([P, TAPS * N], U32, name="w_codes", align_bytes=64)
         w_scales = keep.tile([P, TAPS * N], U8, name="w_scales", align_bytes=64)
-        raw = [[keep.tile([P, 2, c1 - c0], F32, name="raw%d_%d" % (u, c0)) for c0, c1 in LOADS[u]] for u in range(2)]
-        pairs = [keep.tile([P, 2 * T], BF16, name="pairs%d" % u) for u in range(2)]
-        picked = keep.tile([P, 7 * SLICE], U32, name="picked")
+        raw_pair = [keep.tile([P, 2, c1 - c0], F32, name="raw_pair%d" % c0) for c0, c1 in PAIR_LOADS]
+        raw2 = keep.tile([P, T], F32, name="raw2")
+        raw3 = [keep.tile([P, c1 - c0], F32, name="raw3_%d" % c0) for c0, c1 in ROW3_LOADS]
+        pairs = keep.tile([P, 2 * T], BF16, name="pairs")
+        planes = {t: keep.tile([P, T], BF16, name="plane%d" % t) for t in (2, 3)}
         grouped = [keep.tile([P, 4 * SLICE], BF16, name="grouped%d" % s, align_bytes=64) for s in range(SLICES)]
         codes = [keep.tile([P, ROWS * COLS], U32, name="codes%d" % s, align_bytes=64) for s in range(SLICES)]
         scales = [keep.tile([P, ROWS * COLS], U8, name="scales%d" % s, align_bytes=64) for s in range(SLICES)]
         results = [keep.tile([P, 2, SLICE], F32, name="result%d" % s) for s in range(SLICES)]
         banks = [psum.tile([P, 512], F32, name="bank%d" % b) for b in range(2 * SLICES)]
 
-        nc.vector.memset(w_scales[:].bitcast(I32), 0)
+        nc.gpsimd.memset(w_scales[:].bitcast(I32), 0)
         for s in range(SLICES):
             nc.vector.memset(scales[s][:].bitcast(I32), 0)
         nc.vector.memset(codes[0][:].bitcast(I32).rearrange("p (r c) -> p r c", c=COLS)[:, 0:HALO, 0:1], 0)
 
-        def load_x(u, i):
-            c0, c1 = LOADS[u][i]
-            nc.sync.dma_start(out=raw[u][i][:], in_=x_rows[:, 2 * u : 2 * u + 2, c0:c1])
+        def load_pair(i):
+            c0, c1 = PAIR_LOADS[i]
+            nc.sync.dma_start(out=raw_pair[i][:], in_=x_rows[:, 0:2, c0:c1])
+
+        def load_row3(i):
+            c0, c1 = ROW3_LOADS[i]
+            nc.sync.dma_start(out=raw3[i][:], in_=x_rows[:, 3, c0:c1])
 
         def load_scale(n, queue=nc.sync):
             d, q = divmod(n, 4)
@@ -78,47 +86,44 @@ def tile_picked_listconv_relu_e_kernel(
                 in_=words_in[d][0].rearrange("p n t -> p (n t)").bitcast(I32),
             )
 
-        load_x(0, 0)
+        nc.sync.dma_start(out=raw2[:], in_=x_rows[:, 2, :])
         nc.sync.dma_start(offsets[:], offs)
-        for n in range(4, 8):
-            load_scale(n, nc.gpsimd)
-        for n in range(8, 12):
+        load_pair(0)
+        for n in range(4, 9):
             load_scale(n)
-        load_x(0, 1)
-        for i in range(4):
-            load_x(1, i)
-        load_w(1)
-        load_w(2)
+        load_pair(1)
+        load_pair(2)
+        for n in range(9, 12):
+            load_scale(n)
+        for i in range(5):
+            load_row3(i)
+        for d in (1, 2, 0):
+            load_w(d)
         for n in range(0, 4):
             load_scale(n)
-        load_w(0)
 
-        def round_pairs(u, i):
-            c0, c1 = LOADS[u][i]
-            cut = SCALAR_COLS[u][i]
+        def round_pair(i):
+            c0, c1 = PAIR_LOADS[i]
+            cut = PAIR_SCALAR_COLS[i]
             for a, b, on_scalar in ((0, cut, True), (cut, c1 - c0, False)):
-                dst = pairs[u][:, 2 * (c0 + a) : 2 * (c0 + b)].rearrange("p (c i t) -> p c t i", i=4, t=2)
-                src = raw[u][i][:, :, a:b].rearrange("p t (c i) -> p c t i", i=4)
+                if a == b:
+                    continue
+                dst = pairs[:, 2 * (c0 + a) : 2 * (c0 + b)].rearrange("p (c i t) -> p c t i", i=4, t=2)
+                src = raw_pair[i][:, :, a:b].rearrange("p t (c i) -> p c t i", i=4)
                 if on_scalar:
                     nc.scalar.activation(dst, src, COPY)
                 else:
                     nc.vector.tensor_copy(dst, src)
 
-        picked_row = ((2, 3, 0, 1), (4, 5, 6, 3))
+        def gather_pair(s):
+            window = pairs[:].bitcast(U32).indirect(offsets[:, 16 * s : 16 * (s + 1)])
+            dst = grouped[s][:].bitcast(U32).rearrange("p (r c u) -> p u c r", r=PHASES, u=2)[:, 0]
+            nc.vector.tensor_copy(dst, window)
 
-        def gather(u, s, count):
-            window = pairs[u][:].bitcast(U32).indirect(offsets[:, 16 * s : 16 * (s + count)])
-            a = picked_row[u][s] * SLICE
-            nc.vector.tensor_copy(picked[:, a : a + count * SLICE], window)
-
-        def weave(s):
-            r0, r1 = picked_row[0][s], picked_row[1][s]
-            both = picked[:].rearrange("p (k j) -> p k j", j=SLICE)[:, r0 : r1 + 1 : r1 - r0, :]
-            copy = nc.vector.tensor_copy if s == SLICES - 1 else nc.scalar.copy
-            copy(
-                grouped[s][:].bitcast(U32).rearrange("p (r c u) -> p c r u", r=PHASES, u=2),
-                both.rearrange("p u (c r) -> p c r u", r=PHASES),
-            )
+        def gather_plane(t, s):
+            window = planes[t][:].indirect(offsets[:, 16 * s : 16 * (s + 1)])
+            dst = grouped[s][:].rearrange("p (r c t) -> p t c r", r=PHASES, t=4)[:, t]
+            nc.scalar.activation(dst, window, COPY)
 
         def quantise(s):
             for r in (2, 0):
@@ -183,22 +188,24 @@ def tile_picked_listconv_relu_e_kernel(
 
         def finish(s):
             cols = slice(SLICE * s, SLICE * (s + 1))
+            for m in range(2):
+                relu(s, m, (s, m) in VECTOR_RELU)
+                if s == SLICES - 1:
+                    queue = nc.sync if m == 1 else nc.scalar
+                    queue.dma_start(out=out_rows[:, m, cols], in_=results[s][:, m, :])
             if s < SLICES - 1:
-                for m in range(2):
-                    relu(s, m, False)
                 nc.sync.dma_start(out=out_rows[:, :, cols], in_=results[s][:])
-            else:
-                relu(s, 0, False)
-                nc.scalar.dma_start(out=out_rows[:, 0, cols], in_=results[s][:, 0, :])
-                relu(s, 1, True)
-                nc.sync.dma_start(out=out_rows[:, 1, cols], in_=results[s][:, 1, :])
 
-        for i in range(len(LOADS[0])):
-            round_pairs(0, i)
-        for s in range(0, SLICES, 2):
-            gather(0, s, 2)
-        for i in range(len(LOADS[1])):
-            round_pairs(1, i)
+        nc.scalar.activation(planes[2][:, 0:ROW2_SCALAR_COLS], raw2[:, 0:ROW2_SCALAR_COLS], COPY)
+        nc.vector.tensor_copy(planes[2][:, ROW2_SCALAR_COLS:T], raw2[:, ROW2_SCALAR_COLS:T])
+        for s in range(SLICES):
+            gather_plane(2, s)
+        for i in range(len(PAIR_LOADS)):
+            round_pair(i)
+        for s in range(SLICES):
+            gather_pair(s)
+        for i, (c0, c1) in enumerate(ROW3_LOADS):
+            nc.scalar.activation(planes[3][:, c0:c1], raw3[i][:], COPY)
 
         for i in range(WARM):
             nc.tensor.matmul_mx(
@@ -211,17 +218,13 @@ def tile_picked_listconv_relu_e_kernel(
                 stop=True,
             )
 
-        for s in range(3):
-            gather(1, s, 1)
-            weave(s)
+        for s in range(SLICES):
+            gather_plane(3, s)
         for s in range(SLICES):
             quantise(s)
             shift(s)
             multiply(s)
             if s + 1 < SLICES:
                 carry(s)
-            if s == 1:
-                gather(1, 3, 1)
-            if s == 2:
-                weave(3)
+        for s in range(SLICES):
             finish(s)

@@ -24,11 +24,8 @@ COLS = SLICE // PHASES
 HALO = TAPS - 1
 ROWS = HALO + PHASES
 
-PAIR_LOADS = ((0, 1024), (1024, 1536), (1536, 2048))
-PAIR_SCALAR_COLS = (0, 0, 0)
-ROW2_SCALAR_COLS = 640
-ROW3_LOADS = ((0, 512), (512, 1024), (1024, 1536), (1536, 1792), (1792, 2048))
-SPLIT = (0, 3)
+LOADS = (((0, 1536), (1536, 2048)),) + (((0, 1024), (1024, 2048)),) * 2 + (((0, 1024), (1024, 1536), (1536, 2048)),)
+FIRST_SCALAR = (448, 160)
 WARM = 2
 VECTOR_RELU = ((1, 1), (2, 1), (3, 1))
 
@@ -49,11 +46,8 @@ def tile_picked_listconv_relu_e_kernel(
         offsets = keep.tile([P, S // 16], U16, name="offsets")
         w_codes = keep.tile([P, TAPS * N], U32, name="w_codes", align_bytes=64)
         w_scales = keep.tile([P, TAPS * N], U8, name="w_scales", align_bytes=64)
-        raw_pair = [keep.tile([P, 2, c1 - c0], F32, name="raw_pair%d" % c0) for c0, c1 in PAIR_LOADS]
-        raw2 = keep.tile([P, T], F32, name="raw2")
-        raw3 = [keep.tile([P, c1 - c0], F32, name="raw3_%d" % c0) for c0, c1 in ROW3_LOADS]
-        pairs = keep.tile([P, 2 * T], BF16, name="pairs")
-        planes = {t: keep.tile([P, T], BF16, name="plane%d" % t) for t in (2, 3)}
+        raw = [keep.tile([P, T], F32, name="raw%d" % t) for t in range(4)]
+        planes = [keep.tile([P, T], BF16, name="plane%d" % t) for t in range(4)]
         grouped = [keep.tile([P, 4 * SLICE], BF16, name="grouped%d" % s, align_bytes=64) for s in range(SLICES)]
         codes = [keep.tile([P, ROWS * COLS], U32, name="codes%d" % s, align_bytes=64) for s in range(SLICES)]
         scales = [keep.tile([P, ROWS * COLS], U8, name="scales%d" % s, align_bytes=64) for s in range(SLICES)]
@@ -65,13 +59,9 @@ def tile_picked_listconv_relu_e_kernel(
             nc.vector.memset(scales[s][:].bitcast(I32), 0)
         nc.vector.memset(codes[0][:].bitcast(I32).rearrange("p (r c) -> p r c", c=COLS)[:, 0:HALO, 0:1], 0)
 
-        def load_pair(i):
-            c0, c1 = PAIR_LOADS[i]
-            nc.sync.dma_start(out=raw_pair[i][:], in_=x_rows[:, 0:2, c0:c1])
-
-        def load_row3(i):
-            c0, c1 = ROW3_LOADS[i]
-            nc.sync.dma_start(out=raw3[i][:], in_=x_rows[:, 3, c0:c1])
+        def load_x(t, i):
+            c0, c1 = LOADS[t][i]
+            nc.sync.dma_start(out=raw[t][:, c0:c1], in_=x_rows[:, t, c0:c1])
 
         def load_scale(n, queue=nc.sync):
             d, q = divmod(n, 4)
@@ -86,44 +76,41 @@ def tile_picked_listconv_relu_e_kernel(
                 in_=words_in[d][0].rearrange("p n t -> p (n t)").bitcast(I32),
             )
 
-        nc.sync.dma_start(out=raw2[:], in_=x_rows[:, 2, :])
+        load_x(0, 0)
+        load_x(0, 1)
         nc.sync.dma_start(offsets[:], offs)
-        load_pair(0)
-        for n in range(4, 9):
+        load_x(1, 0)
+        for n in range(4, 8):
             load_scale(n)
-        load_pair(1)
-        load_pair(2)
-        for n in range(9, 12):
+        load_x(1, 1)
+        load_x(2, 0)
+        load_x(2, 1)
+        for n in range(8, 12):
             load_scale(n)
-        for i in range(5):
-            load_row3(i)
+        for i in range(3):
+            load_x(3, i)
         for d in (1, 2, 0):
             load_w(d)
         for n in range(0, 4):
             load_scale(n)
 
-        def round_pair(i):
-            c0, c1 = PAIR_LOADS[i]
-            cut = PAIR_SCALAR_COLS[i]
-            for a, b, on_scalar in ((0, cut, True), (cut, c1 - c0, False)):
-                if a == b:
-                    continue
-                dst = pairs[:, 2 * (c0 + a) : 2 * (c0 + b)].rearrange("p (c i t) -> p c t i", i=4, t=2)
-                src = raw_pair[i][:, :, a:b].rearrange("p t (c i) -> p c t i", i=4)
-                if on_scalar:
-                    nc.scalar.activation(dst, src, COPY)
-                else:
-                    nc.vector.tensor_copy(dst, src)
+        def round_x(t, c0, c1):
+            nc.vector.tensor_copy(planes[t][:, c0:c1], raw[t][:, c0:c1])
 
-        def gather_pair(s):
-            window = pairs[:].bitcast(U32).indirect(offsets[:, 16 * s : 16 * (s + 1)])
-            dst = grouped[s][:].bitcast(U32).rearrange("p (r c u) -> p u c r", r=PHASES, u=2)[:, 0]
-            nc.vector.tensor_copy(dst, window)
-
-        def gather_plane(t, s):
-            window = planes[t][:].indirect(offsets[:, 16 * s : 16 * (s + 1)])
+        def gather(t, s, on_vector):
             dst = grouped[s][:].rearrange("p (r c t) -> p t c r", r=PHASES, t=4)[:, t]
-            nc.scalar.activation(dst, window, COPY)
+            picks = offsets[:, 16 * s : 16 * (s + 1)]
+            if on_vector:
+                nc.vector.tensor_copy(dst, raw[t][:].indirect(picks))
+            else:
+                nc.scalar.activation(dst, planes[t][:].indirect(picks), COPY)
+
+        def gather_first(t):
+            gather(t, 0, True)
+
+        def gather_rest(t):
+            for s in range(1, SLICES):
+                gather(t, s, False)
 
         def quantise(s):
             for r in (2, 0):
@@ -163,7 +150,14 @@ def tile_picked_listconv_relu_e_kernel(
             )
 
         def multiply(s):
-            if s in SPLIT:
+            if s == 0:
+                for r in (2, 0):
+                    for m in range(2):
+                        for d in range(1, TAPS):
+                            one_pass(s, m, d, r, 2, r == 2 and d == 1, False)
+                for m in range(2):
+                    one_pass(s, m, 0, 0, PHASES, False, True)
+            elif s == SLICES - 1:
                 for m in range(2):
                     one_pass(s, m, 0, 0, PHASES, True, False)
                     for d in range(1, TAPS):
@@ -191,35 +185,37 @@ def tile_picked_listconv_relu_e_kernel(
             for m in range(2):
                 relu(s, m, (s, m) in VECTOR_RELU)
                 if s == SLICES - 1:
-                    queue = nc.sync if m == 1 else nc.scalar
-                    queue.dma_start(out=out_rows[:, m, cols], in_=results[s][:, m, :])
+                    nc.sync.dma_start(out=out_rows[:, m, cols], in_=results[s][:, m, :])
             if s < SLICES - 1:
                 nc.sync.dma_start(out=out_rows[:, :, cols], in_=results[s][:])
 
-        nc.scalar.activation(planes[2][:, 0:ROW2_SCALAR_COLS], raw2[:, 0:ROW2_SCALAR_COLS], COPY)
-        nc.vector.tensor_copy(planes[2][:, ROW2_SCALAR_COLS:T], raw2[:, ROW2_SCALAR_COLS:T])
-        for s in range(SLICES):
-            gather_plane(2, s)
-        for i in range(len(PAIR_LOADS)):
-            round_pair(i)
-        for s in range(SLICES):
-            gather_pair(s)
-        for i, (c0, c1) in enumerate(ROW3_LOADS):
-            nc.scalar.activation(planes[3][:, c0:c1], raw3[i][:], COPY)
+        for (c0, c1), cut in zip(LOADS[0], FIRST_SCALAR):
+            nc.scalar.activation(planes[0][:, c0 : c0 + cut], raw[0][:, c0 : c0 + cut], COPY)
+            round_x(0, c0 + cut, c1)
+        gather_rest(0)
+        gather_first(0)
+        for t in (1, 2):
+            for c0, c1 in LOADS[t]:
+                round_x(t, c0, c1)
+            gather_rest(t)
+            gather_first(t)
+        for c0, c1 in LOADS[3][:-1]:
+            round_x(3, c0, c1)
+        gather_first(3)
+        round_x(3, *LOADS[3][-1])
 
         for i in range(WARM):
             nc.tensor.matmul_mx(
-                out=banks[7][:],
+                out=banks[7][:, 0:N],
                 lhsT=w_codes[:, N : N + P].bitcast(FP8X4),
                 lhsT_scale=w_scales[:, N : N + P],
-                rhs=w_codes[:, N : 3 * N].bitcast(FP8X4),
-                rhs_scale=w_scales[:, N : 3 * N],
+                rhs=w_codes[:, N : 2 * N].bitcast(FP8X4),
+                rhs_scale=w_scales[:, N : 2 * N],
                 start=True,
                 stop=True,
             )
 
-        for s in range(SLICES):
-            gather_plane(3, s)
+        gather_rest(3)
         for s in range(SLICES):
             quantise(s)
             shift(s)

@@ -22,12 +22,13 @@ SLICES = S // SLICE
 PHASES = 4
 COLS = SLICE // PHASES
 HALO = TAPS - 1
-ROWS = HALO + PHASES
+BLOCKS = tuple((SLICE * s, PHASES) for s in range(SLICES - 1)) + ((S - SLICE, 2), (S - SLICE // 2, 2))
+LAST = len(BLOCKS) - 1
 
+ROW_ORDER = (2, 0, 1, 3)
 LOADS = (((0, 1536), (1536, 2048)),) + (((0, 1024), (1024, 2048)),) * 2 + (((0, 1024), (1024, 1536), (1536, 2048)),)
 FIRST_SCALAR = (448, 160)
-WARM = 2
-VECTOR_RELU = ((1, 1), (2, 1), (3, 1))
+WARM = (N, N, N)
 
 
 def tile_picked_listconv_relu_e_kernel(
@@ -49,18 +50,19 @@ def tile_picked_listconv_relu_e_kernel(
         raw = [keep.tile([P, T], F32, name="raw%d" % t) for t in range(4)]
         planes = [keep.tile([P, T], BF16, name="plane%d" % t) for t in range(4)]
         grouped = [keep.tile([P, 4 * SLICE], BF16, name="grouped%d" % s, align_bytes=64) for s in range(SLICES)]
-        codes = [keep.tile([P, ROWS * COLS], U32, name="codes%d" % s, align_bytes=64) for s in range(SLICES)]
-        scales = [keep.tile([P, ROWS * COLS], U8, name="scales%d" % s, align_bytes=64) for s in range(SLICES)]
-        results = [keep.tile([P, 2, SLICE], F32, name="result%d" % s) for s in range(SLICES)]
+        codes = [keep.tile([P, (HALO + r) * COLS], U32, name="codes%d" % j, align_bytes=64) for j, r in BLOCKS]
+        scales = [keep.tile([P, (HALO + r) * COLS], U8, name="scales%d" % j, align_bytes=64) for j, r in BLOCKS]
+        results = [keep.tile([P, 2, r * COLS], F32, name="result%d" % j) for j, r in BLOCKS]
         banks = [psum.tile([P, 512], F32, name="bank%d" % b) for b in range(2 * SLICES)]
 
         nc.gpsimd.memset(w_scales[:].bitcast(I32), 0)
-        for s in range(SLICES):
-            nc.vector.memset(scales[s][:].bitcast(I32), 0)
+        for tile in scales:
+            nc.vector.memset(tile[:].bitcast(I32), 0)
         nc.vector.memset(codes[0][:].bitcast(I32).rearrange("p (r c) -> p r c", c=COLS)[:, 0:HALO, 0:1], 0)
 
-        def load_x(t, i):
-            c0, c1 = LOADS[t][i]
+        def load_x(n, i):
+            t = ROW_ORDER[n]
+            c0, c1 = LOADS[n][i]
             nc.sync.dma_start(out=raw[t][:, c0:c1], in_=x_rows[:, t, c0:c1])
 
         def load_scale(n, queue=nc.sync):
@@ -98,129 +100,131 @@ def tile_picked_listconv_relu_e_kernel(
             nc.vector.tensor_copy(planes[t][:, c0:c1], raw[t][:, c0:c1])
 
         def gather(t, s, on_vector):
-            dst = grouped[s][:].rearrange("p (r c t) -> p t c r", r=PHASES, t=4)[:, t]
+            phases = BLOCKS[s][1]
+            dst = grouped[s][:].rearrange("p (b r c t) -> p t b c r", r=phases, c=COLS, t=4)[:, t]
             picks = offsets[:, 16 * s : 16 * (s + 1)]
             if on_vector:
                 nc.vector.tensor_copy(dst, raw[t][:].indirect(picks))
             else:
                 nc.scalar.activation(dst, planes[t][:].indirect(picks), COPY)
 
-        def gather_first(t):
-            gather(t, 0, True)
-
-        def gather_rest(t):
-            for s in range(1, SLICES):
-                gather(t, s, False)
-
-        def quantise(s):
-            for r in (2, 0):
+        def quantise(b):
+            first, phases = BLOCKS[b]
+            s, within = divmod(first, SLICE)
+            starts = range(0, phases, 2)
+            for r in starts if b == 0 else reversed(starts):
                 cols = slice((HALO + r) * COLS, (HALO + r + 2) * COLS)
+                a = 4 * (within + COLS * r)
                 nc.vector.quantize_mx(
-                    out=codes[s][:, cols].bitcast(FP8X4),
-                    scales=scales[s][:, cols],
-                    in_=grouped[s][:, 4 * COLS * r : 4 * COLS * (r + 2)],
+                    out=codes[b][:, cols].bitcast(FP8X4),
+                    scales=scales[b][:, cols],
+                    in_=grouped[s][:, a : a + 8 * COLS],
                 )
 
         def rows_of(tile):
             return tile[:].rearrange("p (r c) -> p r c", c=COLS)
 
-        def shift(s):
+        def shift(b):
+            phases = BLOCKS[b][1]
             for tiles in (codes, scales):
-                rows = rows_of(tiles[s])
-                nc.vector.tensor_copy(rows[:, 0:HALO, 1:COLS], rows[:, PHASES:ROWS, 0 : COLS - 1])
+                rows = rows_of(tiles[b])
+                nc.vector.tensor_copy(rows[:, 0:HALO, 1:COLS], rows[:, phases : phases + HALO, 0 : COLS - 1])
 
-        def carry(s):
+        def carry(b):
+            phases = BLOCKS[b][1]
             for tiles in (codes, scales):
                 nc.vector.tensor_copy(
-                    rows_of(tiles[s + 1])[:, 0:HALO, 0:1], rows_of(tiles[s])[:, PHASES:ROWS, COLS - 1 : COLS]
+                    rows_of(tiles[b + 1])[:, 0:HALO, 0:1],
+                    rows_of(tiles[b])[:, phases : phases + HALO, COLS - 1 : COLS],
                 )
 
-        def one_pass(s, m, d, r, count, start, stop):
+        def bank(b, m):
+            return banks[(2 * b + m) % len(banks)]
+
+        def one_pass(b, m, d, r, count, start, stop):
             a = (HALO - d + r) * COLS
             cols = slice(a, a + count * COLS)
             w_cols = slice(d * N + P * m, d * N + P * (m + 1))
             nc.tensor.matmul_mx(
-                out=banks[2 * s + m][:, r * COLS : (r + count) * COLS],
+                out=bank(b, m)[:, r * COLS : (r + count) * COLS],
                 lhsT=w_codes[:, w_cols].bitcast(FP8X4),
                 lhsT_scale=w_scales[:, w_cols],
-                rhs=codes[s][:, cols].bitcast(FP8X4),
-                rhs_scale=scales[s][:, cols],
+                rhs=codes[b][:, cols].bitcast(FP8X4),
+                rhs_scale=scales[b][:, cols],
                 start=start,
                 stop=stop,
             )
 
-        def multiply(s):
-            if s == 0:
-                for r in (2, 0):
+        def multiply(b):
+            if b == 0:
+                order = ((2, 2), (1, 2), (0, 2), (0, 0), (1, 0), (2, 0))
+                for d, r in order[:4]:
                     for m in range(2):
-                        for d in range(1, TAPS):
-                            one_pass(s, m, d, r, 2, r == 2 and d == 1, False)
+                        one_pass(b, m, d, r, 2, (d, r) == order[0], False)
                 for m in range(2):
-                    one_pass(s, m, 0, 0, PHASES, False, True)
-            elif s == SLICES - 1:
-                for m in range(2):
-                    one_pass(s, m, 0, 0, PHASES, True, False)
-                    for d in range(1, TAPS):
-                        one_pass(s, m, d, 2, 2, False, False)
-                for m in range(2):
-                    for d in range(1, TAPS):
-                        one_pass(s, m, d, 0, 2, False, d == TAPS - 1)
+                    for d, r in order[4:]:
+                        one_pass(b, m, d, r, 2, False, (d, r) == order[-1])
             else:
                 for m in range(2):
-                    one_pass(s, m, 0, 0, PHASES, True, False)
-                for m in range(2):
-                    for d in range(1, TAPS):
-                        one_pass(s, m, d, 0, PHASES, False, d == TAPS - 1)
+                    for d in range(TAPS):
+                        one_pass(b, m, d, 0, BLOCKS[b][1], d == 0, d == TAPS - 1)
 
-        def relu(s, m, on_vector):
-            src = banks[2 * s + m][:, 0:SLICE].rearrange("p (r c) -> p c r", r=PHASES)
-            dst = results[s][:, m, :].rearrange("p (c r) -> p c r", r=PHASES)
-            if on_vector:
-                nc.vector.tensor_scalar_max(dst, src, 0.0)
-            else:
-                nc.scalar.activation(dst, src, RELU)
-
-        def finish(s):
-            cols = slice(SLICE * s, SLICE * (s + 1))
+        def finish(b):
+            first, phases = BLOCKS[b]
+            cols = slice(first, first + phases * COLS)
             for m in range(2):
-                relu(s, m, (s, m) in VECTOR_RELU)
-                if s == SLICES - 1:
-                    nc.sync.dma_start(out=out_rows[:, m, cols], in_=results[s][:, m, :])
-            if s < SLICES - 1:
-                nc.sync.dma_start(out=out_rows[:, :, cols], in_=results[s][:])
+                src = bank(b, m)[:, 0 : phases * COLS].rearrange("p (r c) -> p c r", r=phases)
+                dst = results[b][:, m, :].rearrange("p (c r) -> p c r", r=phases)
+                if b == LAST and m == 1:
+                    nc.vector.tensor_scalar_max(dst, src, 0.0)
+                else:
+                    nc.scalar.activation(dst, src, RELU)
+                if b == LAST:
+                    nc.sync.dma_start(out=out_rows[:, m, cols], in_=results[b][:, m, :])
+            if b < LAST:
+                nc.sync.dma_start(out=out_rows[:, :, cols], in_=results[b][:])
 
         for (c0, c1), cut in zip(LOADS[0], FIRST_SCALAR):
-            nc.scalar.activation(planes[0][:, c0 : c0 + cut], raw[0][:, c0 : c0 + cut], COPY)
-            round_x(0, c0 + cut, c1)
-        gather_rest(0)
-        gather_first(0)
-        for t in (1, 2):
-            for c0, c1 in LOADS[t]:
+            nc.scalar.activation(planes[2][:, c0 : c0 + cut], raw[2][:, c0 : c0 + cut], COPY)
+            round_x(2, c0 + cut, c1)
+        for s in range(SLICES):
+            gather(2, s, s == 0)
+        for t in (0, 1):
+            for c0, c1 in LOADS[t + 1]:
                 round_x(t, c0, c1)
-            gather_rest(t)
-            gather_first(t)
+            for s in range(SLICES):
+                gather(t, s, s == SLICES - 1)
         for c0, c1 in LOADS[3][:-1]:
             round_x(3, c0, c1)
-        gather_first(3)
+        gather(3, 0, True)
         round_x(3, *LOADS[3][-1])
 
-        for i in range(WARM):
+        for width in WARM:
             nc.tensor.matmul_mx(
-                out=banks[7][:, 0:N],
+                out=banks[7][:, 0:width],
                 lhsT=w_codes[:, N : N + P].bitcast(FP8X4),
                 lhsT_scale=w_scales[:, N : N + P],
-                rhs=w_codes[:, N : 2 * N].bitcast(FP8X4),
-                rhs_scale=w_scales[:, N : 2 * N],
+                rhs=w_codes[:, N : N + width].bitcast(FP8X4),
+                rhs_scale=w_scales[:, N : N + width],
                 start=True,
                 stop=True,
             )
 
-        gather_rest(3)
-        for s in range(SLICES):
-            quantise(s)
-            shift(s)
-            multiply(s)
-            if s + 1 < SLICES:
-                carry(s)
-        for s in range(SLICES):
-            finish(s)
+        for s in (1, 2):
+            gather(3, s, False)
+        for b in range(len(BLOCKS)):
+            quantise(b)
+            if b == 0:
+                gather(3, SLICES - 1, True)
+            if b == LAST - 1:
+                continue
+            if b == LAST:
+                shift(b - 1)
+                multiply(b - 1)
+                carry(b - 1)
+                finish(b - 1)
+            shift(b)
+            multiply(b)
+            if b < LAST:
+                carry(b)
+            finish(b)

@@ -22,11 +22,11 @@ SLICES = S // SLICE
 PHASES = 4
 COLS = SLICE // PHASES
 HALO = TAPS - 1
-BLOCKS = tuple((SLICE * s, PHASES) for s in range(SLICES - 1)) + ((S - SLICE, 2), (S - SLICE // 2, 2))
+BLOCKS = tuple((SLICE * s, PHASES) for s in range(SLICES))
 LAST = len(BLOCKS) - 1
 
 ROW_ORDER = (2, 0, 1, 3)
-LOADS = (((0, 1536), (1536, 2048)),) + (((0, 1024), (1024, 2048)),) * 2 + (((0, 1024), (1024, 1536), (1536, 2048)),)
+LOADS = (((0, 1536), (1536, 2048)),) + (((0, 1280), (1280, 2048)),) * 2 + (((0, 1024), (1024, 1664), (1664, 2048)),)
 FIRST_SCALAR = (448, 160)
 WARM = (N, N, N)
 
@@ -50,7 +50,7 @@ def tile_picked_listconv_relu_e_kernel(
         raw = [keep.tile([P, T], F32, name="raw%d" % t) for t in range(4)]
         planes = [keep.tile([P, T], BF16, name="plane%d" % t) for t in range(4)]
         grouped = [keep.tile([P, 4 * SLICE], BF16, name="grouped%d" % s, align_bytes=64) for s in range(SLICES)]
-        codes = [keep.tile([P, (HALO + r) * COLS], U32, name="codes%d" % j, align_bytes=64) for j, r in BLOCKS]
+        codes = [keep.tile([P, (HALO + r) * COLS], U32, name="codes%d" % j, align_bytes=64) for j, r in BLOCKS[:2]] * 2
         scales = [keep.tile([P, (HALO + r) * COLS], U8, name="scales%d" % j, align_bytes=64) for j, r in BLOCKS]
         results = [keep.tile([P, 2, r * COLS], F32, name="result%d" % j) for j, r in BLOCKS]
         banks = [psum.tile([P, 512], F32, name="bank%d" % b) for b in range(2 * SLICES)]
@@ -167,7 +167,7 @@ def tile_picked_listconv_relu_e_kernel(
             else:
                 for m in range(2):
                     for d in range(TAPS):
-                        one_pass(b, m, d, 0, BLOCKS[b][1], d == 0, d == TAPS - 1)
+                        one_pass(b, m, d, 0, PHASES, d == 0, d == TAPS - 1)
 
         def finish(b):
             first, phases = BLOCKS[b]
@@ -175,7 +175,7 @@ def tile_picked_listconv_relu_e_kernel(
             for m in range(2):
                 src = bank(b, m)[:, 0 : phases * COLS].rearrange("p (r c) -> p c r", r=phases)
                 dst = results[b][:, m, :].rearrange("p (c r) -> p c r", r=phases)
-                if b == LAST and m == 1:
+                if b == 0 or (b >= 2 and m == 1):
                     nc.vector.tensor_scalar_max(dst, src, 0.0)
                 else:
                     nc.scalar.activation(dst, src, RELU)
@@ -210,21 +210,15 @@ def tile_picked_listconv_relu_e_kernel(
                 stop=True,
             )
 
-        for s in (1, 2):
+        for s in (1, 2, 3):
             gather(3, s, False)
         for b in range(len(BLOCKS)):
             quantise(b)
-            if b == 0:
-                gather(3, SLICES - 1, True)
-            if b == LAST - 1:
-                continue
-            if b == LAST:
-                shift(b - 1)
-                multiply(b - 1)
+            if b > 0:
                 carry(b - 1)
-                finish(b - 1)
             shift(b)
             multiply(b)
-            if b < LAST:
-                carry(b)
-            finish(b)
+            if b > 0 and b != 3:
+                finish(b - 1)
+        finish(2)
+        finish(3)

@@ -22,13 +22,11 @@ SLICES = S // SLICE
 PHASES = 4
 COLS = SLICE // PHASES
 HALO = TAPS - 1
-BLOCKS = tuple((SLICE * s, PHASES) for s in range(SLICES))
-LAST = len(BLOCKS) - 1
+LAST = SLICES - 1
 
-ROW_ORDER = (2, 0, 1, 3)
-LOADS = (((0, 1536), (1536, 2048)),) + (((0, 1280), (1280, 2048)),) * 2 + (((0, 1024), (1024, 1664), (1664, 2048)),)
-FIRST_SCALAR = (448, 160)
-WARM = (N, N, N)
+LOADS = (((0, 1536), (1536, 2048)),) + (((0, 1280), (1280, 2048)),) * 2 + (((0, 1152), (1152, 1792), (1792, 2048)),)
+SCALAR_SHARE = ((448, 160), (0, 0), (0, 0), (0, 0, 0))
+WARM = (512, 512, 512)
 
 
 def tile_picked_listconv_relu_e_kernel(
@@ -42,17 +40,24 @@ def tile_picked_listconv_relu_e_kernel(
 
     with ExitStack() as ctx:
         keep = ctx.enter_context(tc.tile_pool(name="keep", bufs=1))
+        turn = ctx.enter_context(tc.tile_pool(name="turn", bufs=1))
         psum = ctx.enter_context(tc.psum_pool(name="psum", bufs=1))
 
         offsets = keep.tile([P, S // 16], U16, name="offsets")
         w_codes = keep.tile([P, TAPS * N], U32, name="w_codes", align_bytes=64)
         w_scales = keep.tile([P, TAPS * N], U8, name="w_scales", align_bytes=64)
         raw = [keep.tile([P, T], F32, name="raw%d" % t) for t in range(4)]
-        planes = [keep.tile([P, T], BF16, name="plane%d" % t) for t in range(4)]
-        grouped = [keep.tile([P, 4 * SLICE], BF16, name="grouped%d" % s, align_bytes=64) for s in range(SLICES)]
-        codes = [keep.tile([P, (HALO + r) * COLS], U32, name="codes%d" % j, align_bytes=64) for j, r in BLOCKS[:2]] * 2
-        scales = [keep.tile([P, (HALO + r) * COLS], U8, name="scales%d" % j, align_bytes=64) for j, r in BLOCKS]
-        results = [keep.tile([P, 2, r * COLS], F32, name="result%d" % j) for j, r in BLOCKS]
+        planes = [keep.tile([P, T], BF16, name="plane%d" % t, align_bytes=64) for t in range(4)]
+        pairs = [keep.tile([P, 2, SLICE, 2], BF16, name="pairs%d" % s, align_bytes=64) for s in range(SLICES)]
+        grouped = [keep.tile([P, 4 * SLICE], BF16, name="grouped%d" % s, align_bytes=64) for s in range(LAST)]
+        codes = [turn.tile([P, (HALO + PHASES) * COLS], U32, name="codes0", tag="turn", align_bytes=64)]
+        codes.extend(
+            keep.tile([P, (HALO + PHASES) * COLS], U32, name="codes%d" % s, align_bytes=64) for s in range(1, SLICES)
+        )
+        scales = [keep.tile([P, (HALO + PHASES) * COLS], U8, name="scales%d" % s, align_bytes=64) for s in range(SLICES)]
+        warm_codes = keep.tile([P, T // 4], U32, name="warm_codes", align_bytes=64)
+        warm_scales = keep.tile([P, T // 4], U8, name="warm_scales", align_bytes=64)
+        results = [keep.tile([P, 2, SLICE], F32, name="result%d" % s) for s in range(SLICES)]
         banks = [psum.tile([P, 512], F32, name="bank%d" % b) for b in range(2 * SLICES)]
 
         nc.gpsimd.memset(w_scales[:].bitcast(I32), 0)
@@ -60,14 +65,13 @@ def tile_picked_listconv_relu_e_kernel(
             nc.vector.memset(tile[:].bitcast(I32), 0)
         nc.vector.memset(codes[0][:].bitcast(I32).rearrange("p (r c) -> p r c", c=COLS)[:, 0:HALO, 0:1], 0)
 
-        def load_x(n, i):
-            t = ROW_ORDER[n]
-            c0, c1 = LOADS[n][i]
+        def load_x(t, i):
+            c0, c1 = LOADS[t][i]
             nc.sync.dma_start(out=raw[t][:, c0:c1], in_=x_rows[:, t, c0:c1])
 
-        def load_scale(n, queue=nc.sync):
+        def load_scale(n):
             d, q = divmod(n, 4)
-            queue.dma_start(
+            nc.sync.dma_start(
                 out=w_scales[32 * q : 32 * q + 4, d * N : (d + 1) * N].bitcast(I32),
                 in_=scales_in[d][0, 4 * q : 4 * q + 4, :].bitcast(I32),
             )
@@ -87,10 +91,12 @@ def tile_picked_listconv_relu_e_kernel(
         load_x(1, 1)
         load_x(2, 0)
         load_x(2, 1)
-        for n in range(8, 12):
+        for n in range(8, 11):
             load_scale(n)
-        for i in range(3):
-            load_x(3, i)
+        load_x(3, 0)
+        load_scale(11)
+        load_x(3, 1)
+        load_x(3, 2)
         for d in (1, 2, 0):
             load_w(d)
         for n in range(0, 4):
@@ -99,126 +105,140 @@ def tile_picked_listconv_relu_e_kernel(
         def round_x(t, c0, c1):
             nc.vector.tensor_copy(planes[t][:, c0:c1], raw[t][:, c0:c1])
 
-        def gather(t, s, on_vector):
-            phases = BLOCKS[s][1]
-            dst = grouped[s][:].rearrange("p (b r c t) -> p t b c r", r=phases, c=COLS, t=4)[:, t]
+        def gather(t, s):
+            dst = pairs[s][:, t // 2, :, t % 2]
             picks = offsets[:, 16 * s : 16 * (s + 1)]
-            if on_vector:
+            if s == 0:
                 nc.vector.tensor_copy(dst, raw[t][:].indirect(picks))
             else:
                 nc.scalar.activation(dst, planes[t][:].indirect(picks), COPY)
 
-        def quantise(b):
-            first, phases = BLOCKS[b]
-            s, within = divmod(first, SLICE)
-            starts = range(0, phases, 2)
-            for r in starts if b == 0 else reversed(starts):
+        def weave(s, halves, on_vector):
+            src = pairs[s][:].rearrange("p u j e -> p (u j e)").bitcast(U32)
+            src = src.rearrange("p (u c h r) -> p h c r u", u=2, h=2, r=2)[:, halves]
+            dst = grouped[s][:].bitcast(U32).rearrange("p (h r c u) -> p h c r u", h=2, r=2, u=2)[:, halves]
+            if on_vector:
+                nc.vector.tensor_copy(dst, src)
+            else:
+                nc.scalar.copy(dst, src)
+
+        def quantise(s):
+            for r in (0, 2) if s == 0 else (2, 0):
                 cols = slice((HALO + r) * COLS, (HALO + r + 2) * COLS)
-                a = 4 * (within + COLS * r)
+                a = 4 * COLS * r
                 nc.vector.quantize_mx(
-                    out=codes[b][:, cols].bitcast(FP8X4),
-                    scales=scales[b][:, cols],
+                    out=codes[s][:, cols].bitcast(FP8X4),
+                    scales=scales[s][:, cols],
                     in_=grouped[s][:, a : a + 8 * COLS],
                 )
 
         def rows_of(tile):
             return tile[:].rearrange("p (r c) -> p r c", c=COLS)
 
-        def shift(b):
-            phases = BLOCKS[b][1]
+        def shift(s):
             for tiles in (codes, scales):
-                rows = rows_of(tiles[b])
-                nc.vector.tensor_copy(rows[:, 0:HALO, 1:COLS], rows[:, phases : phases + HALO, 0 : COLS - 1])
+                rows = rows_of(tiles[s])
+                nc.vector.tensor_copy(rows[:, 0:HALO, 1:COLS], rows[:, PHASES : PHASES + HALO, 0 : COLS - 1])
 
-        def carry(b):
-            phases = BLOCKS[b][1]
+        def carry(s):
             for tiles in (codes, scales):
                 nc.vector.tensor_copy(
-                    rows_of(tiles[b + 1])[:, 0:HALO, 0:1],
-                    rows_of(tiles[b])[:, phases : phases + HALO, COLS - 1 : COLS],
+                    rows_of(tiles[s + 1])[:, 0:HALO, 0:1],
+                    rows_of(tiles[s])[:, PHASES : PHASES + HALO, COLS - 1 : COLS],
                 )
 
-        def bank(b, m):
-            return banks[(2 * b + m) % len(banks)]
-
-        def one_pass(b, m, d, r, count, start, stop):
+        def one_pass(s, m, d, r, count, start, stop):
             a = (HALO - d + r) * COLS
             cols = slice(a, a + count * COLS)
             w_cols = slice(d * N + P * m, d * N + P * (m + 1))
             nc.tensor.matmul_mx(
-                out=bank(b, m)[:, r * COLS : (r + count) * COLS],
+                out=banks[2 * s + m][:, r * COLS : (r + count) * COLS],
                 lhsT=w_codes[:, w_cols].bitcast(FP8X4),
                 lhsT_scale=w_scales[:, w_cols],
-                rhs=codes[b][:, cols].bitcast(FP8X4),
-                rhs_scale=scales[b][:, cols],
+                rhs=codes[s][:, cols].bitcast(FP8X4),
+                rhs_scale=scales[s][:, cols],
                 start=start,
                 stop=stop,
             )
 
-        def multiply(b):
-            if b == 0:
-                order = ((2, 2), (1, 2), (0, 2), (0, 0), (1, 0), (2, 0))
-                for d, r in order[:4]:
+        def multiply(s):
+            if s == 0:
+                for d in (2, 1):
                     for m in range(2):
-                        one_pass(b, m, d, r, 2, (d, r) == order[0], False)
+                        one_pass(s, m, d, 2, 2, d == 2, False)
+                for r in (2, 0):
+                    for m in range(2):
+                        one_pass(s, m, 0, r, 2, False, False)
                 for m in range(2):
-                    for d, r in order[4:]:
-                        one_pass(b, m, d, r, 2, False, (d, r) == order[-1])
+                    for d in (1, 2):
+                        one_pass(s, m, d, 0, 2, False, d == 2)
+            elif s == LAST:
+                for m in range(2):
+                    one_pass(s, m, 0, 0, PHASES, True, False)
+                    for d in (1, 2):
+                        one_pass(s, m, d, 2, 2, False, False)
+                for m in range(2):
+                    for d in (1, 2):
+                        one_pass(s, m, d, 0, 2, False, d == 2)
             else:
                 for m in range(2):
                     for d in range(TAPS):
-                        one_pass(b, m, d, 0, PHASES, d == 0, d == TAPS - 1)
+                        one_pass(s, m, d, 0, PHASES, d == 0, d == TAPS - 1)
 
-        def finish(b):
-            first, phases = BLOCKS[b]
-            cols = slice(first, first + phases * COLS)
+        def finish(s):
+            cols = slice(SLICE * s, SLICE * (s + 1))
             for m in range(2):
-                src = bank(b, m)[:, 0 : phases * COLS].rearrange("p (r c) -> p c r", r=phases)
-                dst = results[b][:, m, :].rearrange("p (c r) -> p c r", r=phases)
-                if b == 0 or (b >= 2 and m == 1):
+                src = banks[2 * s + m][:, 0:SLICE].rearrange("p (r c) -> p c r", r=PHASES)
+                dst = results[s][:, m, :].rearrange("p (c r) -> p c r", r=PHASES)
+                if (s, m) in ((2, 1), (3, 1)):
                     nc.vector.tensor_scalar_max(dst, src, 0.0)
                 else:
                     nc.scalar.activation(dst, src, RELU)
-                if b == LAST:
-                    nc.sync.dma_start(out=out_rows[:, m, cols], in_=results[b][:, m, :])
-            if b < LAST:
-                nc.sync.dma_start(out=out_rows[:, :, cols], in_=results[b][:])
+                if s == LAST:
+                    nc.sync.dma_start(out=out_rows[:, m, cols], in_=results[s][:, m, :])
+            if s < LAST:
+                nc.sync.dma_start(out=out_rows[:, :, cols], in_=results[s][:])
 
-        for (c0, c1), cut in zip(LOADS[0], FIRST_SCALAR):
-            nc.scalar.activation(planes[2][:, c0 : c0 + cut], raw[2][:, c0 : c0 + cut], COPY)
-            round_x(2, c0 + cut, c1)
-        for s in range(SLICES):
-            gather(2, s, s == 0)
-        for t in (0, 1):
-            for c0, c1 in LOADS[t + 1]:
-                round_x(t, c0, c1)
+        for t in range(4):
+            for (c0, c1), cut in zip(LOADS[t], SCALAR_SHARE[t]):
+                if cut:
+                    nc.scalar.activation(planes[t][:, c0 : c0 + cut], raw[t][:, c0 : c0 + cut], COPY)
+                round_x(t, c0 + cut, c1)
             for s in range(SLICES):
-                gather(t, s, s == SLICES - 1)
-        for c0, c1 in LOADS[3][:-1]:
-            round_x(3, c0, c1)
-        gather(3, 0, True)
-        round_x(3, *LOADS[3][-1])
+                gather(t, s)
 
+        nc.vector.quantize_mx(out=warm_codes[:].bitcast(FP8X4), scales=warm_scales[:], in_=planes[0][:])
         for width in WARM:
             nc.tensor.matmul_mx(
                 out=banks[7][:, 0:width],
-                lhsT=w_codes[:, N : N + P].bitcast(FP8X4),
-                lhsT_scale=w_scales[:, N : N + P],
-                rhs=w_codes[:, N : N + width].bitcast(FP8X4),
-                rhs_scale=w_scales[:, N : N + width],
+                lhsT=warm_codes[:, 0:P].bitcast(FP8X4),
+                lhsT_scale=w_scales[:, 2 * N : 2 * N + P],
+                rhs=warm_codes[:, 0:width].bitcast(FP8X4),
+                rhs_scale=warm_scales[:, 0:width],
                 start=True,
                 stop=True,
             )
 
-        for s in (1, 2, 3):
-            gather(3, s, False)
-        for b in range(len(BLOCKS)):
-            quantise(b)
-            if b > 0:
-                carry(b - 1)
-            shift(b)
-            multiply(b)
-            if b > 0 and b != 3:
-                finish(b - 1)
-        finish(2)
-        finish(3)
+        weave(0, slice(0, 1), True)
+        weave(0, slice(1, 2), True)
+        quantise(0)
+        weave(1, slice(0, 2), True)
+        shift(0)
+        multiply(0)
+        weave(2, slice(0, 2), False)
+        quantise(1)
+        carry(0)
+        shift(1)
+        multiply(1)
+        finish(0)
+        grouped.append(turn.tile([P, 4 * SLICE], BF16, name="grouped3", tag="turn", align_bytes=64))
+        weave(3, slice(1, 2), False)
+        for s in (2, 3):
+            quantise(s)
+            carry(s - 1)
+            shift(s)
+            multiply(s)
+            if s == 2:
+                weave(3, slice(0, 1), True)
+            finish(s - 1)
+        finish(LAST)

@@ -26,7 +26,7 @@ LAST = SLICES - 1
 
 LOADS = (((0, 1536), (1536, 2048)),) + (((0, 1280), (1280, 2048)),) * 2 + (((0, 1152), (1152, 1792), (1792, 2048)),)
 SCALAR_SHARE = ((448, 160), (0, 0), (0, 0), (0, 0, 0))
-WARM = (512, 512, 512)
+WARM = (N, N, 2 * N)
 
 
 def tile_picked_listconv_relu_e_kernel(
@@ -40,23 +40,17 @@ def tile_picked_listconv_relu_e_kernel(
 
     with ExitStack() as ctx:
         keep = ctx.enter_context(tc.tile_pool(name="keep", bufs=1))
-        turn = ctx.enter_context(tc.tile_pool(name="turn", bufs=1))
         psum = ctx.enter_context(tc.psum_pool(name="psum", bufs=1))
 
         offsets = keep.tile([P, S // 16], U16, name="offsets")
         w_codes = keep.tile([P, TAPS * N], U32, name="w_codes", align_bytes=64)
         w_scales = keep.tile([P, TAPS * N], U8, name="w_scales", align_bytes=64)
         raw = [keep.tile([P, T], F32, name="raw%d" % t) for t in range(4)]
-        planes = [keep.tile([P, T], BF16, name="plane%d" % t, align_bytes=64) for t in range(4)]
-        pairs = [keep.tile([P, 2, SLICE, 2], BF16, name="pairs%d" % s, align_bytes=64) for s in range(SLICES)]
-        grouped = [keep.tile([P, 4 * SLICE], BF16, name="grouped%d" % s, align_bytes=64) for s in range(LAST)]
-        codes = [turn.tile([P, (HALO + PHASES) * COLS], U32, name="codes0", tag="turn", align_bytes=64)]
-        codes.extend(
-            keep.tile([P, (HALO + PHASES) * COLS], U32, name="codes%d" % s, align_bytes=64) for s in range(1, SLICES)
-        )
+        planes = [keep.tile([P, T], BF16, name="plane%d" % t) for t in range(4)]
+        pairs = {s: keep.tile([P, 2, SLICE, 2], BF16, name="pairs%d" % s, align_bytes=64) for s in range(1, SLICES)}
+        grouped = [keep.tile([P, 4 * SLICE], BF16, name="grouped%d" % s, align_bytes=64) for s in range(2)] * 2
+        codes = [keep.tile([P, (HALO + PHASES) * COLS], U32, name="codes%d" % s, align_bytes=64) for s in range(SLICES)]
         scales = [keep.tile([P, (HALO + PHASES) * COLS], U8, name="scales%d" % s, align_bytes=64) for s in range(SLICES)]
-        warm_codes = keep.tile([P, T // 4], U32, name="warm_codes", align_bytes=64)
-        warm_scales = keep.tile([P, T // 4], U8, name="warm_scales", align_bytes=64)
         results = [keep.tile([P, 2, SLICE], F32, name="result%d" % s) for s in range(SLICES)]
         banks = [psum.tile([P, 512], F32, name="bank%d" % b) for b in range(2 * SLICES)]
 
@@ -91,12 +85,10 @@ def tile_picked_listconv_relu_e_kernel(
         load_x(1, 1)
         load_x(2, 0)
         load_x(2, 1)
-        for n in range(8, 11):
+        for n in range(8, 12):
             load_scale(n)
-        load_x(3, 0)
-        load_scale(11)
-        load_x(3, 1)
-        load_x(3, 2)
+        for i in range(3):
+            load_x(3, i)
         for d in (1, 2, 0):
             load_w(d)
         for n in range(0, 4):
@@ -106,12 +98,12 @@ def tile_picked_listconv_relu_e_kernel(
             nc.vector.tensor_copy(planes[t][:, c0:c1], raw[t][:, c0:c1])
 
         def gather(t, s):
-            dst = pairs[s][:, t // 2, :, t % 2]
             picks = offsets[:, 16 * s : 16 * (s + 1)]
             if s == 0:
+                dst = grouped[0][:].rearrange("p (r c t) -> p t c r", r=PHASES, t=4)[:, t]
                 nc.vector.tensor_copy(dst, raw[t][:].indirect(picks))
             else:
-                nc.scalar.activation(dst, planes[t][:].indirect(picks), COPY)
+                nc.scalar.activation(pairs[s][:, t // 2, :, t % 2], planes[t][:].indirect(picks), COPY)
 
         def weave(s, halves, on_vector):
             src = pairs[s][:].rearrange("p u j e -> p (u j e)").bitcast(U32)
@@ -172,7 +164,7 @@ def tile_picked_listconv_relu_e_kernel(
                 for m in range(2):
                     for d in (1, 2):
                         one_pass(s, m, d, 0, 2, False, d == 2)
-            elif s == LAST:
+            elif s < LAST:
                 for m in range(2):
                     one_pass(s, m, 0, 0, PHASES, True, False)
                     for d in (1, 2):
@@ -194,9 +186,9 @@ def tile_picked_listconv_relu_e_kernel(
                     nc.vector.tensor_scalar_max(dst, src, 0.0)
                 else:
                     nc.scalar.activation(dst, src, RELU)
-                if s == LAST:
+                if s != 1:
                     nc.sync.dma_start(out=out_rows[:, m, cols], in_=results[s][:, m, :])
-            if s < LAST:
+            if s == 1:
                 nc.sync.dma_start(out=out_rows[:, :, cols], in_=results[s][:])
 
         for t in range(4):
@@ -207,38 +199,35 @@ def tile_picked_listconv_relu_e_kernel(
             for s in range(SLICES):
                 gather(t, s)
 
-        nc.vector.quantize_mx(out=warm_codes[:].bitcast(FP8X4), scales=warm_scales[:], in_=planes[0][:])
         for width in WARM:
             nc.tensor.matmul_mx(
                 out=banks[7][:, 0:width],
-                lhsT=warm_codes[:, 0:P].bitcast(FP8X4),
-                lhsT_scale=w_scales[:, 2 * N : 2 * N + P],
-                rhs=warm_codes[:, 0:width].bitcast(FP8X4),
-                rhs_scale=warm_scales[:, 0:width],
+                lhsT=w_codes[:, N : N + P].bitcast(FP8X4),
+                lhsT_scale=w_scales[:, N : N + P],
+                rhs=w_codes[:, N : N + width].bitcast(FP8X4),
+                rhs_scale=w_scales[:, N : N + width],
                 start=True,
                 stop=True,
             )
 
-        weave(0, slice(0, 1), True)
-        weave(0, slice(1, 2), True)
+        weave(1, slice(1, 2), True)
         quantise(0)
-        weave(1, slice(0, 2), True)
+        weave(1, slice(0, 1), True)
         shift(0)
         multiply(0)
-        weave(2, slice(0, 2), False)
+        weave(2, slice(1, 2), False)
         quantise(1)
+        weave(2, slice(0, 1), True)
         carry(0)
         shift(1)
         multiply(1)
         finish(0)
-        grouped.append(turn.tile([P, 4 * SLICE], BF16, name="grouped3", tag="turn", align_bytes=64))
-        weave(3, slice(1, 2), False)
         for s in (2, 3):
             quantise(s)
+            if s == 2:
+                weave(3, slice(0, 2), True)
             carry(s - 1)
             shift(s)
             multiply(s)
-            if s == 2:
-                weave(3, slice(0, 1), True)
             finish(s - 1)
         finish(LAST)

@@ -24,9 +24,9 @@ COLS = SLICE // PHASES
 HALO = TAPS - 1
 LAST = SLICES - 1
 
-LOADS = (((0, 1536), (1536, 2048)),) + (((0, 1280), (1280, 2048)),) * 2 + (((0, 1152), (1152, 1792), (1792, 2048)),)
-SCALAR_SHARE = ((448, 160), (0, 0), (0, 0), (0, 0, 0))
-WARM = (N, N, 2 * N)
+LOADS = (((0, 2048),),) + (((0, 1280), (1280, 2048)),) * 2 + (((0, 1152), (1152, 1792), (1792, 2048)),)
+SCALAR_SHARE = ((640,), (0, 0), (0, 0), (0, 0, 0))
+WARM = (N, N, N)
 
 
 def tile_picked_listconv_relu_e_kernel(
@@ -77,20 +77,19 @@ def tile_picked_listconv_relu_e_kernel(
             )
 
         load_x(0, 0)
-        load_x(0, 1)
         nc.sync.dma_start(offsets[:], offs)
         load_x(1, 0)
+        load_x(1, 1)
         for n in range(4, 8):
             load_scale(n)
-        load_x(1, 1)
-        load_x(2, 0)
-        load_x(2, 1)
+        for t in (2, 3):
+            for i in range(len(LOADS[t])):
+                load_x(t, i)
+        load_w(1)
         for n in range(8, 12):
             load_scale(n)
-        for i in range(3):
-            load_x(3, i)
-        for d in (1, 2, 0):
-            load_w(d)
+        load_w(2)
+        load_w(0)
         for n in range(0, 4):
             load_scale(n)
 
@@ -158,20 +157,18 @@ def tile_picked_listconv_relu_e_kernel(
                 for d in (2, 1):
                     for m in range(2):
                         one_pass(s, m, d, 2, 2, d == 2, False)
-                for r in (2, 0):
+                for d in (1, 2):
                     for m in range(2):
-                        one_pass(s, m, 0, r, 2, False, False)
+                        one_pass(s, m, d, 0, 2, False, False)
                 for m in range(2):
-                    for d in (1, 2):
-                        one_pass(s, m, d, 0, 2, False, d == 2)
+                    for r in (2, 0):
+                        one_pass(s, m, 0, r, 2, False, r == 0)
             elif s < LAST:
                 for m in range(2):
                     one_pass(s, m, 0, 0, PHASES, True, False)
-                    for d in (1, 2):
-                        one_pass(s, m, d, 2, 2, False, False)
                 for m in range(2):
                     for d in (1, 2):
-                        one_pass(s, m, d, 0, 2, False, d == 2)
+                        one_pass(s, m, d, 0, PHASES, False, d == 2)
             else:
                 for m in range(2):
                     for d in range(TAPS):

@@ -24,8 +24,8 @@ COLS = SLICE // PHASES
 HALO = TAPS - 1
 LAST = SLICES - 1
 
-LOADS = (((0, 2048),),) + (((0, 1280), (1280, 2048)),) * 2 + (((0, 1152), (1152, 1792), (1792, 2048)),)
-SCALAR_SHARE = ((640,), (0, 0), (0, 0), (0, 0, 0))
+LOADS = (((0, 1536), (1536, 2048)),) + (((0, 1408), (1408, 2048)),) * 2 + (((0, 1152), (1152, 1664), (1664, 2048)),)
+SCALAR_SHARE = ((448, 96), (0, 0), (0, 0), (0, 0, 0))
 WARM = (N, N, N)
 
 
@@ -77,6 +77,7 @@ def tile_picked_listconv_relu_e_kernel(
             )
 
         load_x(0, 0)
+        load_x(0, 1)
         nc.sync.dma_start(offsets[:], offs)
         load_x(1, 0)
         load_x(1, 1)
@@ -212,9 +213,8 @@ def tile_picked_listconv_relu_e_kernel(
         weave(1, slice(0, 1), True)
         shift(0)
         multiply(0)
-        weave(2, slice(1, 2), False)
         quantise(1)
-        weave(2, slice(0, 1), True)
+        weave(2, slice(0, 2), True)
         carry(0)
         shift(1)
         multiply(1)

@@ -26,7 +26,7 @@ LAST = SLICES - 1
 
 LOADS = (((0, 1536), (1536, 2048)),) + (((0, 1408), (1408, 2048)),) * 2 + (((0, 1152), (1152, 1664), (1664, 2048)),)
 SCALAR_SHARE = ((448, 96), (0, 0), (0, 0), (0, 0, 0))
-WARM = (N, N, N)
+WARM = (N, N, 2 * N)
 
 
 def tile_picked_listconv_relu_e_kernel(
@@ -81,15 +81,15 @@ def tile_picked_listconv_relu_e_kernel(
         nc.sync.dma_start(offsets[:], offs)
         load_x(1, 0)
         load_x(1, 1)
-        for n in range(4, 8):
+        for n in range(4, 9):
             load_scale(n)
         for t in (2, 3):
             for i in range(len(LOADS[t])):
                 load_x(t, i)
         load_w(1)
-        for n in range(8, 12):
-            load_scale(n)
         load_w(2)
+        for n in range(9, 12):
+            load_scale(n)
         load_w(0)
         for n in range(0, 4):
             load_scale(n)

@@ -23,10 +23,7 @@ PHASES = 4
 COLS = SLICE // PHASES
 HALO = TAPS - 1
 LAST = SLICES - 1
-
-LOADS = (((0, 1536), (1536, 2048)),) + (((0, 1408), (1408, 2048)),) * 2 + (((0, 1152), (1152, 1664), (1664, 2048)),)
-SCALAR_SHARE = ((448, 96), (0, 0), (0, 0), (0, 0, 0))
-WARM = (N, N, 2 * N)
+WARM = (N, N)
 
 
 def tile_picked_listconv_relu_e_kernel(
@@ -46,29 +43,34 @@ def tile_picked_listconv_relu_e_kernel(
         w_codes = keep.tile([P, TAPS * N], U32, name="w_codes", align_bytes=64)
         w_scales = keep.tile([P, TAPS * N], U8, name="w_scales", align_bytes=64)
         raw = [keep.tile([P, T], F32, name="raw%d" % t) for t in range(4)]
-        planes = [keep.tile([P, T], BF16, name="plane%d" % t) for t in range(4)]
-        pairs = {s: keep.tile([P, 2, SLICE, 2], BF16, name="pairs%d" % s, align_bytes=64) for s in range(1, SLICES)}
-        grouped = [keep.tile([P, 4 * SLICE], BF16, name="grouped%d" % s, align_bytes=64) for s in range(2)] * 2
+        picked = {
+            (s, u): keep.tile([P, 2 * SLICE], BF16, name="picked%d%d" % (s, u), align_bytes=64)
+            for s in range(1, SLICES)
+            for u in range(2)
+        }
+        grouped = [keep.tile([P, 4 * SLICE], BF16, name="grouped%d" % s, align_bytes=64) for s in range(SLICES)]
         codes = [keep.tile([P, (HALO + PHASES) * COLS], U32, name="codes%d" % s, align_bytes=64) for s in range(SLICES)]
         scales = [keep.tile([P, (HALO + PHASES) * COLS], U8, name="scales%d" % s, align_bytes=64) for s in range(SLICES)]
         results = [keep.tile([P, 2, SLICE], F32, name="result%d" % s) for s in range(SLICES)]
         banks = [psum.tile([P, 512], F32, name="bank%d" % b) for b in range(2 * SLICES)]
 
+        idle = keep.tile([P, 2], F32, name="idle")
+        nc.gpsimd.memset(idle[:, 0:1], 0.0)
+        nc.scalar.activation(idle[:, 1:2], idle[:, 0:1], COPY)
         nc.gpsimd.memset(w_scales[:].bitcast(I32), 0)
         for tile in scales:
             nc.vector.memset(tile[:].bitcast(I32), 0)
         nc.vector.memset(codes[0][:].bitcast(I32).rearrange("p (r c) -> p r c", c=COLS)[:, 0:HALO, 0:1], 0)
 
-        def load_x(t, i):
-            c0, c1 = LOADS[t][i]
-            nc.sync.dma_start(out=raw[t][:, c0:c1], in_=x_rows[:, t, c0:c1])
+        def load_x(t):
+            nc.sync.dma_start(out=raw[t][:], in_=x_rows[:, t, :])
 
-        def load_scale(n):
-            d, q = divmod(n, 4)
-            nc.sync.dma_start(
-                out=w_scales[32 * q : 32 * q + 4, d * N : (d + 1) * N].bitcast(I32),
-                in_=scales_in[d][0, 4 * q : 4 * q + 4, :].bitcast(I32),
-            )
+        def load_scales(d):
+            for q in range(4):
+                nc.sync.dma_start(
+                    out=w_scales[32 * q : 32 * q + 4, d * N : (d + 1) * N].bitcast(I32),
+                    in_=scales_in[d][0, 4 * q : 4 * q + 4, :].bitcast(I32),
+                )
 
         def load_w(d):
             nc.sync.dma_start(
@@ -76,43 +78,31 @@ def tile_picked_listconv_relu_e_kernel(
                 in_=words_in[d][0].rearrange("p n t -> p (n t)").bitcast(I32),
             )
 
-        load_x(0, 0)
-        load_x(0, 1)
+        load_x(0)
         nc.sync.dma_start(offsets[:], offs)
-        load_x(1, 0)
-        load_x(1, 1)
-        for n in range(4, 9):
-            load_scale(n)
-        for t in (2, 3):
-            for i in range(len(LOADS[t])):
-                load_x(t, i)
+        load_x(1)
+        load_scales(1)
+        load_x(2)
+        load_x(3)
         load_w(1)
+        load_scales(2)
         load_w(2)
-        for n in range(9, 12):
-            load_scale(n)
         load_w(0)
-        for n in range(0, 4):
-            load_scale(n)
-
-        def round_x(t, c0, c1):
-            nc.vector.tensor_copy(planes[t][:, c0:c1], raw[t][:, c0:c1])
+        load_scales(0)
 
         def gather(t, s):
-            picks = offsets[:, 16 * s : 16 * (s + 1)]
+            looked_up = raw[t][:].indirect(offsets[:, 16 * s : 16 * (s + 1)])
             if s == 0:
                 dst = grouped[0][:].rearrange("p (r c t) -> p t c r", r=PHASES, t=4)[:, t]
-                nc.vector.tensor_copy(dst, raw[t][:].indirect(picks))
+                nc.vector.tensor_copy(dst, looked_up)
             else:
-                nc.scalar.activation(pairs[s][:, t // 2, :, t % 2], planes[t][:].indirect(picks), COPY)
+                e = t % 2
+                nc.scalar.activation(picked[s, t // 2][:, e * SLICE : (e + 1) * SLICE], looked_up, COPY)
 
-        def weave(s, halves, on_vector):
-            src = pairs[s][:].rearrange("p u j e -> p (u j e)").bitcast(U32)
-            src = src.rearrange("p (u c h r) -> p h c r u", u=2, h=2, r=2)[:, halves]
-            dst = grouped[s][:].bitcast(U32).rearrange("p (h r c u) -> p h c r u", h=2, r=2, u=2)[:, halves]
-            if on_vector:
-                nc.vector.tensor_copy(dst, src)
-            else:
-                nc.scalar.copy(dst, src)
+        def lay(s, u, halves):
+            src = picked[s, u][:].rearrange("p (e c h r) -> p h c r e", e=2, h=2, r=2)[:, halves]
+            dst = grouped[s][:].rearrange("p (h r c u e) -> p u h c r e", h=2, r=2, u=2, e=2)[:, u, halves]
+            nc.vector.tensor_copy(dst, src)
 
         def quantise(s):
             for r in (0, 2) if s == 0 else (2, 0):
@@ -190,12 +180,11 @@ def tile_picked_listconv_relu_e_kernel(
                 nc.sync.dma_start(out=out_rows[:, :, cols], in_=results[s][:])
 
         for t in range(4):
-            for (c0, c1), cut in zip(LOADS[t], SCALAR_SHARE[t]):
-                if cut:
-                    nc.scalar.activation(planes[t][:, c0 : c0 + cut], raw[t][:, c0 : c0 + cut], COPY)
-                round_x(t, c0 + cut, c1)
             for s in range(SLICES):
                 gather(t, s)
+            if t == 1:
+                for s in range(1, SLICES):
+                    lay(s, 0, slice(0, 2))
 
         for width in WARM:
             nc.tensor.matmul_mx(
@@ -208,13 +197,13 @@ def tile_picked_listconv_relu_e_kernel(
                 stop=True,
             )
 
-        weave(1, slice(1, 2), True)
+        lay(1, 1, slice(1, 2))
         quantise(0)
-        weave(1, slice(0, 1), True)
+        lay(1, 1, slice(0, 1))
         shift(0)
         multiply(0)
         quantise(1)
-        weave(2, slice(0, 2), True)
+        lay(2, 1, slice(0, 2))
         carry(0)
         shift(1)
         multiply(1)
@@ -222,7 +211,7 @@ def tile_picked_listconv_relu_e_kernel(
         for s in (2, 3):
             quantise(s)
             if s == 2:
-                weave(3, slice(0, 2), True)
+                lay(3, 1, slice(0, 2))
             carry(s - 1)
             shift(s)
             multiply(s)

@@ -23,7 +23,7 @@ PHASES = 4
 COLS = SLICE // PHASES
 HALO = TAPS - 1
 LAST = SLICES - 1
-WARM = (N, N)
+WARM = ((P, N), (P, N), (32, P), (32, P), (32, P))
 
 
 def tile_picked_listconv_relu_e_kernel(
@@ -186,11 +186,11 @@ def tile_picked_listconv_relu_e_kernel(
                 for s in range(1, SLICES):
                     lay(s, 0, slice(0, 2))
 
-        for width in WARM:
+        for rows, width in WARM:
             nc.tensor.matmul_mx(
-                out=banks[7][:, 0:width],
-                lhsT=w_codes[:, N : N + P].bitcast(FP8X4),
-                lhsT_scale=w_scales[:, N : N + P],
+                out=banks[7][0:rows, 0:width],
+                lhsT=w_codes[:, N : N + rows].bitcast(FP8X4),
+                lhsT_scale=w_scales[:, N : N + rows],
                 rhs=w_codes[:, N : N + width].bitcast(FP8X4),
                 rhs_scale=w_scales[:, N : N + width],
                 start=True,

@@ -65,8 +65,8 @@ def tile_picked_listconv_relu_e_kernel(
         def load_x(t):
             nc.sync.dma_start(out=raw[t][:], in_=x_rows[:, t, :])
 
-        def load_scales(d):
-            for q in range(4):
+        def load_scales(d, quadrants=range(4)):
+            for q in quadrants:
                 nc.sync.dma_start(
                     out=w_scales[32 * q : 32 * q + 4, d * N : (d + 1) * N].bitcast(I32),
                     in_=scales_in[d][0, 4 * q : 4 * q + 4, :].bitcast(I32),
@@ -81,9 +81,10 @@ def tile_picked_listconv_relu_e_kernel(
         load_x(0)
         nc.sync.dma_start(offsets[:], offs)
         load_x(1)
-        load_scales(1)
+        load_scales(1, range(3))
         load_x(2)
         load_x(3)
+        load_scales(1, range(3, 4))
         load_w(1)
         load_scales(2)
         load_w(2)
@@ -110,7 +111,7 @@ def tile_picked_listconv_relu_e_kernel(
                 a = 4 * COLS * r
                 nc.vector.quantize_mx(
                     out=codes[s][:, cols].bitcast(FP8X4),
-                    scales=scales[s][:, cols],
+                    scales=scales[s][4:P, cols],
                     in_=grouped[s][:, a : a + 8 * COLS],
                 )
 
@@ -138,7 +139,7 @@ def tile_picked_listconv_relu_e_kernel(
                 lhsT=w_codes[:, w_cols].bitcast(FP8X4),
                 lhsT_scale=w_scales[:, w_cols],
                 rhs=codes[s][:, cols].bitcast(FP8X4),
-                rhs_scale=scales[s][:, cols],
+                rhs_scale=scales[s][4:P, cols],
                 start=start,
                 stop=stop,
             )
@@ -174,10 +175,7 @@ def tile_picked_listconv_relu_e_kernel(
                     nc.vector.tensor_scalar_max(dst, src, 0.0)
                 else:
                     nc.scalar.activation(dst, src, RELU)
-                if s != 1:
-                    nc.sync.dma_start(out=out_rows[:, m, cols], in_=results[s][:, m, :])
-            if s == 1:
-                nc.sync.dma_start(out=out_rows[:, :, cols], in_=results[s][:])
+                nc.sync.dma_start(out=out_rows[:, m, cols], in_=results[s][:, m, :])
 
         for t in range(4):
             for s in range(SLICES):

@@ -91,18 +91,18 @@ def tile_picked_listconv_relu_e_kernel(
         load_w(0)
         load_scales(0)
 
-        def gather(t, s):
-            looked_up = raw[t][:].indirect(offsets[:, 16 * s : 16 * (s + 1)])
+        def gather(t, s, j0=0, j1=SLICE):
+            looked_up = raw[t][:].indirect(offsets[:, (SLICE * s + j0) // 16 : (SLICE * s + j1) // 16])
             if s == 0:
                 dst = grouped[0][:].rearrange("p (r c t) -> p t c r", r=PHASES, t=4)[:, t]
                 nc.vector.tensor_copy(dst, looked_up)
             else:
-                e = t % 2
-                nc.scalar.activation(picked[s, t // 2][:, e * SLICE : (e + 1) * SLICE], looked_up, COPY)
+                plane = picked[s, t // 2][:, t % 2 * SLICE + j0 : t % 2 * SLICE + j1]
+                nc.scalar.activation(plane, looked_up, COPY)
 
-        def lay(s, u, halves):
-            src = picked[s, u][:].rearrange("p (e c h r) -> p h c r e", e=2, h=2, r=2)[:, halves]
-            dst = grouped[s][:].rearrange("p (h r c u e) -> p u h c r e", h=2, r=2, u=2, e=2)[:, u, halves]
+        def lay(s, u, c0=0, c1=COLS):
+            src = picked[s, u][:].rearrange("p (e c h r) -> p h c r e", e=2, h=2, r=2)[:, :, c0:c1]
+            dst = grouped[s][:].rearrange("p (h r c u e) -> p u h c r e", h=2, r=2, u=2, e=2)[:, u, :, c0:c1]
             nc.vector.tensor_copy(dst, src)
 
         def quantise(s):
@@ -179,10 +179,14 @@ def tile_picked_listconv_relu_e_kernel(
 
         for t in range(4):
             for s in range(SLICES):
-                gather(t, s)
+                if (t, s) == (3, 1):
+                    gather(t, s, 0, SLICE // 2)
+                    gather(t, s, SLICE // 2, SLICE)
+                else:
+                    gather(t, s)
             if t == 1:
                 for s in range(1, SLICES):
-                    lay(s, 0, slice(0, 2))
+                    lay(s, 0)
 
         for rows, width in WARM:
             nc.tensor.matmul_mx(
@@ -195,13 +199,13 @@ def tile_picked_listconv_relu_e_kernel(
                 stop=True,
             )
 
-        lay(1, 1, slice(1, 2))
+        lay(1, 1, 0, COLS // 2)
         quantise(0)
-        lay(1, 1, slice(0, 1))
+        lay(1, 1, COLS // 2, COLS)
         shift(0)
         multiply(0)
         quantise(1)
-        lay(2, 1, slice(0, 2))
+        lay(2, 1)
         carry(0)
         shift(1)
         multiply(1)
@@ -209,7 +213,7 @@ def tile_picked_listconv_relu_e_kernel(
         for s in (2, 3):
             quantise(s)
             if s == 2:
-                lay(3, 1, slice(0, 2))
+                lay(3, 1)
             carry(s - 1)
             shift(s)
             multiply(s)

@@ -42,7 +42,6 @@ def tile_picked_listconv_relu_e_kernel(
         offsets = keep.tile([P, S // 16], U16, name="offsets")
         w_codes = keep.tile([P, TAPS * N], U32, name="w_codes", align_bytes=64)
         w_scales = keep.tile([P, TAPS * N], U8, name="w_scales", align_bytes=64)
-        raw = [keep.tile([P, T], F32, name="raw%d" % t) for t in range(4)]
         picked = {
             (s, u): keep.tile([P, 2 * SLICE], BF16, name="picked%d%d" % (s, u), align_bytes=64)
             for s in range(1, SLICES)
@@ -51,7 +50,8 @@ def tile_picked_listconv_relu_e_kernel(
         grouped = [keep.tile([P, 4 * SLICE], BF16, name="grouped%d" % s, align_bytes=64) for s in range(SLICES)]
         codes = [keep.tile([P, (HALO + PHASES) * COLS], U32, name="codes%d" % s, align_bytes=64) for s in range(SLICES)]
         scales = [keep.tile([P, (HALO + PHASES) * COLS], U8, name="scales%d" % s, align_bytes=64) for s in range(SLICES)]
-        results = [keep.tile([P, 2, SLICE], F32, name="result%d" % s) for s in range(SLICES)]
+        raw = [keep.tile([P, T], F32, name="raw%d" % t, align_bytes=256) for t in range(4)]
+        results = [keep.tile([P, 2, SLICE], F32, name="result%d" % s, align_bytes=256) for s in range(SLICES)]
         banks = [psum.tile([P, 512], F32, name="bank%d" % b) for b in range(2 * SLICES)]
 
         idle = keep.tile([P, 2], F32, name="idle")

@@ -39,9 +39,8 @@ def tile_picked_listconv_relu_e_kernel(
         keep = ctx.enter_context(tc.tile_pool(name="keep", bufs=1))
         psum = ctx.enter_context(tc.psum_pool(name="psum", bufs=1))
 
-        offsets = keep.tile([P, S // 16], U16, name="offsets")
-        w_codes = keep.tile([P, TAPS * N], U32, name="w_codes", align_bytes=64)
-        w_scales = keep.tile([P, TAPS * N], U8, name="w_scales", align_bytes=64)
+        w_codes = keep.tile([P, TAPS * N], U32, name="w_codes", align_bytes=256)
+        w_scales = keep.tile([P, TAPS * N], U8, name="w_scales", align_bytes=256)
         picked = {
             (s, u): keep.tile([P, 2 * SLICE], BF16, name="picked%d%d" % (s, u), align_bytes=64)
             for s in range(1, SLICES)
@@ -50,8 +49,9 @@ def tile_picked_listconv_relu_e_kernel(
         grouped = [keep.tile([P, 4 * SLICE], BF16, name="grouped%d" % s, align_bytes=64) for s in range(SLICES)]
         codes = [keep.tile([P, (HALO + PHASES) * COLS], U32, name="codes%d" % s, align_bytes=64) for s in range(SLICES)]
         scales = [keep.tile([P, (HALO + PHASES) * COLS], U8, name="scales%d" % s, align_bytes=64) for s in range(SLICES)]
-        raw = [keep.tile([P, T], F32, name="raw%d" % t, align_bytes=256) for t in range(4)]
-        results = [keep.tile([P, 2, SLICE], F32, name="result%d" % s, align_bytes=256) for s in range(SLICES)]
+        offsets = keep.tile([P, S // 16], U16, name="offsets", align_bytes=256)
+        raw = [keep.tile([P, T], F32, name="raw%d" % t, align_bytes=1024) for t in range(4)]
+        results = [keep.tile([P, 2, SLICE], F32, name="result%d" % s, align_bytes=1024) for s in range(SLICES)]
         banks = [psum.tile([P, 512], F32, name="bank%d" % b) for b in range(2 * SLICES)]
 
         idle = keep.tile([P, 2], F32, name="idle")

@@ -45,9 +45,13 @@ def tile_picked_listconv_relu_e_kernel(
             (s, u): keep.tile([P, 2 * SLICE], BF16, name="picked%d%d" % (s, u), align_bytes=64)
             for s in range(1, SLICES)
             for u in range(2)
+            if (s, u) != (LAST, 1)
         }
-        grouped = [keep.tile([P, 4 * SLICE], BF16, name="grouped%d" % s, align_bytes=64) for s in range(SLICES)]
-        codes = [keep.tile([P, (HALO + PHASES) * COLS], U32, name="codes%d" % s, align_bytes=64) for s in range(SLICES)]
+        grouped = [
+            keep.tile([P, 4 * SLICE], BF16, name="grouped%d" % s, tag="slice%d" % s, align_bytes=64)
+            for s in range(SLICES)
+        ]
+        codes = [keep.tile([P, (HALO + PHASES) * COLS], U32, name="codes%d" % s, align_bytes=64) for s in range(LAST)]
         scales = [keep.tile([P, (HALO + PHASES) * COLS], U8, name="scales%d" % s, align_bytes=64) for s in range(SLICES)]
         offsets = keep.tile([P, S // 16], U16, name="offsets", align_bytes=256)
         raw = [keep.tile([P, T], F32, name="raw%d" % t, align_bytes=1024) for t in range(4)]
@@ -93,9 +97,11 @@ def tile_picked_listconv_relu_e_kernel(
 
         def gather(t, s, j0=0, j1=SLICE):
             looked_up = raw[t][:].indirect(offsets[:, (SLICE * s + j0) // 16 : (SLICE * s + j1) // 16])
+            in_place = grouped[s][:].rearrange("p (r c t) -> p t c r", r=PHASES, t=4)[:, t]
             if s == 0:
-                dst = grouped[0][:].rearrange("p (r c t) -> p t c r", r=PHASES, t=4)[:, t]
-                nc.vector.tensor_copy(dst, looked_up)
+                nc.vector.tensor_copy(in_place, looked_up)
+            elif (s, t // 2) == (LAST, 1):
+                nc.scalar.activation(in_place, looked_up, COPY)
             else:
                 plane = picked[s, t // 2][:, t % 2 * SLICE + j0 : t % 2 * SLICE + j1]
                 nc.scalar.activation(plane, looked_up, COPY)
@@ -211,9 +217,13 @@ def tile_picked_listconv_relu_e_kernel(
         multiply(1)
         finish(0)
         for s in (2, 3):
+            if s == LAST:
+                codes.append(
+                    keep.tile(
+                        [P, (HALO + PHASES) * COLS], U32, name="codes%d" % s, tag="slice%d" % (s - 1), align_bytes=64
+                    )
+                )
             quantise(s)
-            if s == 2:
-                lay(3, 1)
             carry(s - 1)
             shift(s)
             multiply(s)

from contextlib import ExitStack

import concourse.mybir as mybir

K, T, S, N = 512, 2048, 1024, 256
TAPS = 3
FLOPS = 2 * TAPS * K * N * S

F32 = mybir.dt.float32
BF16 = mybir.dt.bfloat16
I32 = mybir.dt.int32
U32 = mybir.dt.uint32
U16 = mybir.dt.uint16
U8 = mybir.dt.uint8
FP8X4 = mybir.dt.float8_e4m3fn_x4
COPY = mybir.ActivationFunctionType.Copy
RELU = mybir.ActivationFunctionType.Relu

P = 128
SLICE = 256
SLICES = S // SLICE
PHASES = 4
COLS = SLICE // PHASES
HALO = TAPS - 1
LAST = SLICES - 1
WARM = ((P, N), (P, N), (32, P), (32, P), (32, P))


def tile_picked_listconv_relu_e_kernel(
    tc, xT, w1_words, w1_scales, w2_words, w2_scales, w3_words, w3_scales, offs, out
):
    nc = tc.nc
    words_in = (w1_words, w2_words, w3_words)
    scales_in = (w1_scales, w2_scales, w3_scales)
    x_rows = xT.rearrange("(p j) t -> p j t", j=4)
    out_rows = out.rearrange("(m p) s -> p m s", p=P)

    with ExitStack() as ctx:
        keep = ctx.enter_context(tc.tile_pool(name="keep", bufs=1))
        psum = ctx.enter_context(tc.psum_pool(name="psum", bufs=1))

        w_codes = keep.tile([P, TAPS * N], U32, name="w_codes", align_bytes=256)
        w_scales = keep.tile([P, TAPS * N], U8, name="w_scales", align_bytes=256)
        picked = {
            (s, u): keep.tile([P, 2 * SLICE], BF16, name="picked%d%d" % (s, u), align_bytes=64)
            for s in range(1, SLICES)
            for u in range(2)
            if (s, u) != (LAST, 1)
        }
        grouped = [
            keep.tile([P, 4 * SLICE], BF16, name="grouped%d" % s, tag="slice%d" % s, align_bytes=64)
            for s in range(SLICES)
        ]
        codes = [keep.tile([P, (HALO + PHASES) * COLS], U32, name="codes%d" % s, align_bytes=64) for s in range(LAST)]
        scales = [keep.tile([P, (HALO + PHASES) * COLS], U8, name="scales%d" % s, align_bytes=64) for s in range(SLICES)]
        offsets = keep.tile([P, S // 16], U16, name="offsets", align_bytes=256)
        raw = [keep.tile([P, T], F32, name="raw%d" % t, align_bytes=1024) for t in range(4)]
        results = [keep.tile([P, 2, SLICE], F32, name="result%d" % s, align_bytes=1024) for s in range(SLICES)]
        banks = [psum.tile([P, 512], F32, name="bank%d" % b) for b in range(2 * SLICES)]

        idle = keep.tile([P, 2], F32, name="idle")
        nc.gpsimd.memset(idle[:, 0:1], 0.0)
        nc.scalar.activation(idle[:, 1:2], idle[:, 0:1], COPY)
        nc.gpsimd.memset(w_scales[:].bitcast(I32), 0)
        for tile in scales:
            nc.vector.memset(tile[:].bitcast(I32), 0)
        nc.vector.memset(codes[0][:].bitcast(I32).rearrange("p (r c) -> p r c", c=COLS)[:, 0:HALO, 0:1], 0)

        def load_x(t):
            nc.sync.dma_start(out=raw[t][:], in_=x_rows[:, t, :])

        def load_scales(d, quadrants=range(4)):
            for q in quadrants:
                nc.sync.dma_start(
                    out=w_scales[32 * q : 32 * q + 4, d * N : (d + 1) * N].bitcast(I32),
                    in_=scales_in[d][0, 4 * q : 4 * q + 4, :].bitcast(I32),
                )

        def load_w(d):
            nc.sync.dma_start(
                out=w_codes[:, d * N : (d + 1) * N].bitcast(I32),
                in_=words_in[d][0].rearrange("p n t -> p (n t)").bitcast(I32),
            )

        load_x(0)
        nc.sync.dma_start(offsets[:], offs)
        load_x(1)
        load_scales(1, range(3))
        load_x(2)
        load_x(3)
        load_scales(1, range(3, 4))
        load_w(1)
        load_scales(2)
        load_w(2)
        load_w(0)
        load_scales(0)

        def gather(t, s, j0=0, j1=SLICE):
            looked_up = raw[t][:].indirect(offsets[:, (SLICE * s + j0) // 16 : (SLICE * s + j1) // 16])
            in_place = grouped[s][:].rearrange("p (r c t) -> p t c r", r=PHASES, t=4)[:, t]
            if s == 0:
                nc.vector.tensor_copy(in_place, looked_up)
            elif (s, t // 2) == (LAST, 1):
                nc.scalar.activation(in_place, looked_up, COPY)
            else:
                plane = picked[s, t // 2][:, t % 2 * SLICE + j0 : t % 2 * SLICE + j1]
                nc.scalar.activation(plane, looked_up, COPY)

        def lay(s, u, c0=0, c1=COLS):
            src = picked[s, u][:].rearrange("p (e c h r) -> p h c r e", e=2, h=2, r=2)[:, :, c0:c1]
            dst = grouped[s][:].rearrange("p (h r c u e) -> p u h c r e", h=2, r=2, u=2, e=2)[:, u, :, c0:c1]
            nc.vector.tensor_copy(dst, src)

        def quantise(s):
            for r in (0, 2) if s == 0 else (2, 0):
                cols = slice((HALO + r) * COLS, (HALO + r + 2) * COLS)
                a = 4 * COLS * r
                nc.vector.quantize_mx(
                    out=codes[s][:, cols].bitcast(FP8X4),
                    scales=scales[s][4:P, cols],
                    in_=grouped[s][:, a : a + 8 * COLS],
                )

        def rows_of(tile):
            return tile[:].rearrange("p (r c) -> p r c", c=COLS)

        def shift(s):
            for tiles in (codes, scales):
                rows = rows_of(tiles[s])
                nc.vector.tensor_copy(rows[:, 0:HALO, 1:COLS], rows[:, PHASES : PHASES + HALO, 0 : COLS - 1])

        def carry(s):
            for tiles in (codes, scales):
                nc.vector.tensor_copy(
                    rows_of(tiles[s + 1])[:, 0:HALO, 0:1],
                    rows_of(tiles[s])[:, PHASES : PHASES + HALO, COLS - 1 : COLS],
                )

        def one_pass(s, m, d, r, count, start, stop):
            a = (HALO - d + r) * COLS
            cols = slice(a, a + count * COLS)
            w_cols = slice(d * N + P * m, d * N + P * (m + 1))
            nc.tensor.matmul_mx(
                out=banks[2 * s + m][:, r * COLS : (r + count) * COLS],
                lhsT=w_codes[:, w_cols].bitcast(FP8X4),
                lhsT_scale=w_scales[:, w_cols],
                rhs=codes[s][:, cols].bitcast(FP8X4),
                rhs_scale=scales[s][4:P, cols],
                start=start,
                stop=stop,
            )

        def multiply(s):
            if s == 0:
                for d in (2, 1):
                    for m in range(2):
                        one_pass(s, m, d, 2, 2, d == 2, False)
                for d in (1, 2):
                    for m in range(2):
                        one_pass(s, m, d, 0, 2, False, False)
                for m in range(2):
                    for r in (2, 0):
                        one_pass(s, m, 0, r, 2, False, r == 0)
            elif s < LAST:
                for m in range(2):
                    one_pass(s, m, 0, 0, PHASES, True, False)
                for m in range(2):
                    for d in (1, 2):
                        one_pass(s, m, d, 0, PHASES, False, d == 2)
            else:
                for m in range(2):
                    for d in range(TAPS):
                        one_pass(s, m, d, 0, PHASES, d == 0, d == TAPS - 1)

        def finish(s):
            cols = slice(SLICE * s, SLICE * (s + 1))
            for m in range(2):
                src = banks[2 * s + m][:, 0:SLICE].rearrange("p (r c) -> p c r", r=PHASES)
                dst = results[s][:, m, :].rearrange("p (c r) -> p c r", r=PHASES)
                if (s, m) in ((2, 1), (3, 1)):
                    nc.vector.tensor_scalar_max(dst, src, 0.0)
                else:
                    nc.scalar.activation(dst, src, RELU)
                nc.sync.dma_start(out=out_rows[:, m, cols], in_=results[s][:, m, :])

        for t in range(4):
            for s in range(SLICES):
                if (t, s) == (3, 1):
                    gather(t, s, 0, SLICE // 2)
                    gather(t, s, SLICE // 2, SLICE)
                else:
                    gather(t, s)
            if t == 1:
                for s in range(1, SLICES):
                    lay(s, 0)

        for rows, width in WARM:
            nc.tensor.matmul_mx(
                out=banks[7][0:rows, 0:width],
                lhsT=w_codes[:, N : N + rows].bitcast(FP8X4),
                lhsT_scale=w_scales[:, N : N + rows],
                rhs=w_codes[:, N : N + width].bitcast(FP8X4),
                rhs_scale=w_scales[:, N : N + width],
                start=True,
                stop=True,
            )

        lay(1, 1, 0, COLS // 2)
        quantise(0)
        lay(1, 1, COLS // 2, COLS)
        shift(0)
        multiply(0)
        quantise(1)
        lay(2, 1)
        carry(0)
        shift(1)
        multiply(1)
        finish(0)
        for s in (2, 3):
            if s == LAST:
                codes.append(
                    keep.tile(
                        [P, (HALO + PHASES) * COLS], U32, name="codes%d" % s, tag="slice%d" % (s - 1), align_bytes=64
                    )
                )
            quantise(s)
            carry(s - 1)
            shift(s)
            multiply(s)
            finish(s - 1)
        finish(LAST)
